import numpy as np, ml_dtypes
CORES = [9,25,41,57]
N = 4
BF = ml_dtypes.bfloat16
def gentries(a):
    return np.ascontiguousarray(a.reshape(8, 16, -1).transpose(0, 2, 1)).reshape(8, -1)
def gtable(e):
    e = np.asarray(e); return np.ascontiguousarray(e.reshape(8, -1, 16).transpose(0, 2, 1)).reshape(128, -1).astype(np.int32)
V, K, A, B, R = 2048, 16, 4, 4, 4
LR = V // R
LOW = 0.0625
def parts(rng):
    s = LOW + (1.0 - LOW) * rng.random((N, 8, 16, V)); nb = rng.integers(0, V, (N, 8, R, K, LR))
    tr = np.where(rng.random((N, 8, 1, V)) < 0.5, rng.integers(1, 16, (N, 8, K, V)), rng.integers(10, 16, (N, 8, K, V)))
    return s, nb, tr, rng.integers(0, V, (N, 8, V)), rng.integers(0, V, (N, 8, V))
def kinds(rng, n):
    return (np.arange(N)[:, None] + np.arange(8) + rng.integers(0, n)) % n
def pack(s, nb, tr, ex, pt):
    return {"sat": np.clip(s.reshape(N, 128, V).astype(np.float32), np.float32(LOW), np.float32(1)), "nb": np.stack([gtable(a.reshape(8, -1)) for a in nb]),
            "tr": np.ascontiguousarray(tr.reshape(N, 8 * K, V)).astype(np.float32).astype(BF), "ex": np.ascontiguousarray(ex).astype(np.int32), "pt": np.ascontiguousarray(pt).astype(np.int32)}
def setup_inputs(rng):
    return pack(*parts(rng))
def setup_inputs_spread(rng):
    s, nb, tr, ex, pt = parts(rng)
    s = np.exp2(-4.0 * rng.random((N, 8, 1, V))) * (0.5 + 0.5 * rng.random((N, 8, 16, V)))
    tr = np.minimum(np.floor(np.exp2(4.0 * rng.random(tr.shape))), 15).astype(np.int64)
    nb = np.minimum((V * rng.random(nb.shape) ** 3).astype(np.int64), V - 1); nb[:, 1::2] = V - 1 - nb[:, 1::2]
    ex = np.minimum((V * rng.random(ex.shape) ** 2).astype(np.int64), V - 1); pt = V - 1 - np.minimum((V * rng.random(pt.shape) ** 2).astype(np.int64), V - 1)
    return pack(s, nb, tr, ex, pt)
def tips(rng, a):
    return np.where(rng.random(a.shape) < 0.75, (V - 1) * rng.integers(0, 2, a.shape), a)
def setup_inputs_ends(rng):
    s, nb, tr, ex, pt = parts(rng); nb = tips(rng, nb); ex = tips(rng, ex); pt = tips(rng, pt); tr = 1 + 14 * rng.integers(0, 2, tr.shape)
    s = np.where(rng.random((N, 8, 1, V)) < 0.75, np.where(rng.random(s.shape) < 0.5, LOW, 1.0), s)
    for c in (0, V - 1):
        s[:, :, 12:, c] = 1.0; s[:, :, :4, c] = LOW; s[:, :, 4:12, c] = np.where(rng.random((N, 8, 8)) < 0.5, LOW, 1.0)
        ex[:, :, c] = (V - 1) * rng.integers(0, 2, (N, 8)); pt[:, :, c] = (V - 1) * rng.integers(0, 2, (N, 8))
        nb[:, :, c // LR, :, c % LR] = (V - 1) * rng.integers(0, 2, (N, 8, K))
    nb[N - 1, 7, R - 1, 1, LR - 1] = 0; nb[N - 1, 7, R - 1, K - 1, LR - 1] = V - 1
    tr[N - 1, 7, :, V - 1] = 1; tr[N - 1, 7, 1, V - 1] = 15; tr[N - 1, 7, K - 1, V - 1] = 15
    tr[N - 1, 7, :, V - 2] = 1; tr[N - 1, 7, K - 1, V - 2] = 15
    return pack(s, nb, tr, ex, pt)
def setup_inputs_corners(rng):
    s, nb, tr, ex, pt = parts(rng); kd = kinds(rng, 4)
    s[:, :, 1:8] = s[:, :, :1]; s[:, :, 9:] = s[:, :, 8:9]; s[..., V - LR + 1::2] = s[..., V - LR::2]
    m = kd == 0; own = np.arange(V).reshape(R, 1, LR)
    nb[m] = np.where(np.arange(K)[:, None] % 2 == 0, own, rng.choice(np.array([0, V - 2, V - 1]), nb[m].shape)); ex[m] = np.arange(V); pt[m] = rng.choice(np.array([0, V - 1]), pt[m].shape)
    m = kd == 1; n = nb[m].shape[0]
    nb[m] = V - 1 - rng.integers(0, 4, nb[m].shape); ex[m] = np.where(rng.random((n, V)) < 0.5, V - 1 - rng.integers(0, 4, (n, V)), ex[m])
    pt[m] = V - 1 - rng.integers(0, 2, (n, V)); tr[m] = 1 + 14 * rng.integers(0, 2, (n, 1, V))
    m = kd == 2; v = nb[m]; v[:, :, 0:K - 1:2] = rng.integers(V - LR, V, v[:, :, 0:K - 1:2].shape); v[:, :, 1::2] = v[:, :, 0:K - 1:2] ^ 1
    nb[m] = v; tr[m] = 1 + 14 * rng.integers(0, 2, (v.shape[0], 1, V))
    m = kd == 3; ex[m] = (np.arange(V) + 1) % V; pt[m] = rng.choice(np.array([0, 1, V - 2, V - 1]), pt[m].shape)
    n = nb[m].shape[0]; e = V - LR + 2 * rng.integers(0, LR // 2, n); sm = s[m]; sm[np.arange(n), :, e] = 1.0; sm[np.arange(n), :, e + 1] = 0.5; s[m] = sm
    kk = np.arange(K)[:, None]; j = rng.integers(0, K, (n, 1, V)); i = (j + 1 + rng.integers(0, K - 1, (n, 1, V))) % K; hit = (rng.random((n, 1, V)) < 0.5) & (np.arange(V) < V - LR)
    v = nb[m].transpose(0, 2, 1, 3).reshape(n, K, V); v = np.where(hit & (kk == j), e[:, None, None], np.where(hit & (kk == i), e[:, None, None] + 1, v))
    nb[m] = v.reshape(n, K, R, LR).transpose(0, 2, 1, 3)
    tr[m] = np.where(hit, np.where(kk == j, 3, np.where(kk == i, 8, rng.integers(1, 3, (n, K, V)))), tr[m])
    return pack(s, nb, tr, ex, pt)
def setup_inputs_crowd(rng):
    s, nb, tr, ex, pt = parts(rng); kd = kinds(rng, 4); p = int(rng.integers(1, 16)); odd = s[:, :, p].copy()
    s[:, :, 1:] = s[:, :, :1].copy(); s[:, :, p] = odd
    m = kd == 0; n = nb[m].shape[0]; nb[m] = rng.integers(0, V, (n, 1, 1, 1)); pt[m] = rng.integers(0, V, (n, 1))
    m = kd == 1; n = nb[m].shape[0]; few = rng.integers(0, V, (n, 4))
    nb[m] = few[np.arange(n)[:, None, None, None], rng.integers(0, 4, (n, R, K, LR))]; tr[m] = rng.integers(1, 16, (n, 1, V))
    m = kd == 2; n = nb[m].shape[0]; j = rng.integers(0, K, (n, 1, V)); kk = np.arange(K)[:, None]; tr[m] = np.where(kk == j, 15, 1)
    m = kd == 3; n = nb[m].shape[0]; j = rng.integers(0, K, (n, 1, V)); i = (j + 1 + rng.integers(0, K - 1, (n, 1, V))) % K; tr[m] = np.where((kk == j) | (kk == i), 15, 1)
    return pack(s, nb, tr, ex, pt)
THIRD = (11183600, 11183900, 2048, -25)
BANDS = ((2 ** 23, 2 ** 24 - 16, 16, -27), (2 ** 23, 2 ** 24 - 16, 16, -26), THIRD, THIRD, THIRD, (13421773, 2 ** 24 - 8, 8, -25), (2 ** 23, 2 ** 24 - 2 ** 20, 4, -24), (15770584, 2 ** 24 - 4, 4, -24))
def setup_inputs_calm(rng):
    s, nb, tr, ex, pt = parts(rng); kd = kinds(rng, 2)
    for p, (lo, hi, wd, e) in enumerate(BANDS): s[:, :, p] = (rng.integers(lo, hi) + rng.integers(0, wd, (N, 8, V))) * 2.0 ** e
    tr[:] = rng.integers(1, 16, (N, 8, 1, V))
    m = kd == 0; n = nb[m].shape[0]; nb[m] = rng.integers(0, 4, nb[m].shape)
    ex[m] = np.where(rng.random((n, V)) < 0.5, rng.integers(0, 4, (n, V)), ex[m]); pt[m] = np.where(rng.random((n, V)) < 0.5, rng.integers(0, 4, (n, V)), pt[m])
    return pack(s, nb, tr, ex, pt)
def check_inputs(d):
    bad = []
    for k, lo, hi in (("sat", LOW, 1), ("nb", 0, V - 1), ("tr", 1, 15), ("ex", 0, V - 1), ("pt", 0, V - 1)):
        a = np.asarray(d[k]).astype(np.float64)
        if not (np.min(a) >= lo and np.max(a) <= hi): bad.append("range of " + k)
        elif k == "tr" and np.any(a != np.floor(a)): bad.append("whole numbers in " + k)
    return bad
ONE, TWO, THREE, HALF = np.float32(1), np.float32(2), np.float32(3), np.float32(0.5)
def flow(s):
    return (s * s) * (THREE - TWO * s)
def step(y, s):
    return s + HALF * (flow(y) - flow(s))
def pick(w, ix):
    return np.take_along_axis(w, ix[:, :, None, :], 3)
def reference(sat, nb, tr, ex, pt):
    s = sat.astype(np.float32).reshape(N, 8, 16, V); x = ex.astype(np.int64); po = pt.astype(np.int64)
    cand = np.stack([gentries(a) for a in nb]).astype(np.int64).reshape(N, 8, R, K, LR); w = tr.astype(np.float32).reshape(N, 8, K, R, LR)
    for t in range(R):
        lo = t * LR
        c = [np.zeros((N, 8, 1), np.int64) + np.arange(lo, lo + LR)]
        for j in range(A - 1): c.append(np.take_along_axis(x, c[-1], 2))
        sf = np.roll(s, (-1, -t), (0, 1)); xf = np.roll(x, (-1, -t), (0, 1))
        d = [np.take_along_axis(po, c[-1], 2)]
        for j in range(B - 1): d.append(np.take_along_axis(xf, d[-1], 2))
        y = pick(sf, d[B - 1])
        for j in range(B - 2, -1, -1): y = step(y, pick(sf, d[j]))
        for j in range(A - 1, -1, -1): y = step(y, pick(s, c[j]))
        s[..., lo:lo + LR] = y
        n = cand[:, :, t]
        u = pick(s, n.reshape(N, 8, K * LR)).reshape(N, 8, 16, K, LR)
        v = ONE - u
        q = w[:, :, :, t][:, :, None] * (u * u + HALF * (v * v))
        k = np.argmax(q, axis=3)
        votes = np.sum((k[:, :, :, None, :] == np.arange(K)[:, None]).astype(np.int64), axis=2)
        win = np.argmax(votes, axis=2)
        x[..., lo:lo + LR] = np.take_along_axis(n, win[:, :, None], 2)[:, :, 0]
    return {"ys": s.reshape(N, 128, V), "yx": x.astype(np.float32)}

@@ -1,0 +1,545 @@
+from concourse.bass import DstId, RemoteDMATransfer
+from concourse.mybir import AluOpType, ActivationFunctionType
+
+V, K, R, LR = 2048, 16, 4, 512
+NCH = 4
+CW = V // (2 * NCH)
+URING = 6
+CH = [(0, 192), (192, 352), (352, 512)]
+F32, BF, I32, U16 = "float32", "bfloat16", "int32", "uint16"
+
+SCRATCH = {}
+for _n in ("S", "F", "H", "SN", "FN", "FX", "Q", "XO", "NBF"):
+    SCRATCH[_n] = ("sbuf", [128, V], F32)
+SCRATCH.update({
+    "XI": ("sbuf", [128, V], BF), "NBI": ("sbuf", [128, V], I32), "NBU": ("sbuf", [128, V], U16),
+    "TR": ("sbuf", [128, V], BF), "U": ("sbuf", [128, URING * LR], F32), "M": ("sbuf", [128, 15 * LR], F32),
+    "Z": ("sbuf", [128, 15 * LR], BF), "GV": ("sbuf", [128, 10 * LR], F32), "XN": ("sbuf", [128, V], BF), "Y": ("sbuf", [128, LR], F32),
+    "TB": ("sbuf", [128, LR], F32), "TD": ("sbuf", [128, LR], F32), "TA": ("sbuf", [128, LR], F32),
+    "G0": ("sbuf", [128, LR], BF), "G1": ("sbuf", [128, LR], BF), "LS": ("sbuf", [128, 6 * 32], U16),
+    "EXW": ("sbuf", [128, 128], U16), "EXN": ("sbuf", [128, 128], U16), "NXO": ("sbuf", [128, 128], U16),
+    "NXN": ("sbuf", [128, 128], U16), "EC": ("sbuf", [128, 384], I32), "EF": ("sbuf", [128, 384], F32),
+    "EH": ("sbuf", [128, 768], BF), "XP": ("sbuf", [128, V], BF),
+    "W2": ("sbuf", [128, 256], BF), "I0": ("sbuf", [128, 256], I32), "I1": ("sbuf", [128, 256], I32),
+    "I2": ("sbuf", [128, 256], I32), "I3": ("sbuf", [128, 176], I32), "PI": ("sbuf", [128, 8], I32),
+    "PF": ("sbuf", [128, 8], F32), "VB": ("sbuf", [128, 256], BF), "W0": ("sbuf", [128, 256], BF),
+    "W1": ("sbuf", [128, 256], BF), "RB": ("sbuf", [128, 176], F32), "IDB": ("sbuf", [128, 384], BF),
+    "BO": ("sbuf", [128, 128], BF), "BS": ("sbuf", [128, 16 * 128], BF), "KC": ("sbuf", [128, LR], BF),
+    "RM": ("sbuf", [128, LR], BF), "CS": ("sbuf", [128, LR], BF), "BM": ("sbuf", [128, LR], F32),
+    "XA": ("sbuf", [128, 32], I32), "XB": ("sbuf", [128, 32], I32),
+})
+for _b in range(8):
+    SCRATCH["B%d" % _b] = ("psum", [128, 512], F32)
+
+SEMAPHORES = (["cv", "ca", "cp", "cg", "lex", "lpt", "xd", "ln0", "ln1", "ltr", "outs", "lsi", "lsr",
+               "aex"] + ["ls%d" % j for j in range(NCH)] + ["ad%d" % j for j in range(NCH)]
+              + ["ah%d" % j for j in range(NCH)] + ["hh%d" % j for j in range(NCH)]
+              + ["sf%d" % t for t in range(3)] + ["nx%d" % t for t in range(3)] + ["cr%d" % t for t in range(3)])
+
+ADD, SUB, MUL, MAX = AluOpType.add, AluOpType.subtract, AluOpType.mult, AluOpType.max
+AND, SHR, EQ, GE = AluOpType.bitwise_and, AluOpType.arith_shift_right, AluOpType.is_equal, AluOpType.is_ge
+SQ, IDF, CPY = ActivationFunctionType.Square, ActivationFunctionType.Identity, ActivationFunctionType.Copy
+
+
+def bits(m):
+    return bin(m).count("1")
+
+
+def helpers_of(c, dst, T, topo):
+    free = [h for h in topo.cores_of(c) if T.rank_of(h) is None and topo.may_write(h, dst) and topo.addr(h)[2] != topo.addr(c)[2]]
+    hs = [[h for h in free if topo.die(h) == topo.die(c)][0], [h for h in free if topo.die(h) != topo.die(c)][0]]
+    es = topo.engines(c, hs[0])
+    return hs, [sum(1 << e for e in es[0::2]), sum(1 << e for e in es[1::2])]
+
+
+def helper_program(g, core, half, n_in, dst, T, topo):
+    rid, pid, _ = topo.addr(dst)
+    m = topo.mask(core, dst)
+    for j in range(NCH):
+        lo = half * (V // 2) + j * CW
+        g.wait_ge(T.sem["hh%d" % j], n_in)
+        g.remote_dma(T.SN[:, lo:lo + CW], T.S[:, lo:lo + CW], T.sem[("ad%d", "ah%d")[half] % j], T.sem.lsi, pid, rid, m)
+    g.wait_ge(T.sem.lsi, NCH * bits(m))
+
+
+def rank_program(g, core, T, topo):
+    rank = T.rank_of(core)
+    n = len(T.cores)
+    if rank is None:
+        for r in range(n):
+            hs, ms = helpers_of(T.cores[r], T.cores[(r - 1) % n], T, topo)
+            if core in hs:
+                h = hs.index(core)
+                helper_program(g, core, h, bits(ms[h]), T.cores[(r - 1) % n], T, topo)
+        return
+    pred, succ = T.cores[(rank - 1) % n], T.cores[(rank + 1) % n]
+    hs, hm = helpers_of(core, pred, T, topo)
+    hid = [DstId(rid=topo.addr(h)[0], pnc=topo.addr(h)[1]) for h in hs]
+    prid, ppid, _ = topo.addr(pred)
+    srid, spid, _ = topo.addr(succ)
+    pm = topo.mask(core, pred)
+    pe = topo.engines(core, pred)
+    pm_a = sum(1 << e for e in pe[:len(pe) // 2])
+    pm_b = pm & ~pm_a
+    n_s = bits(topo.mask(succ, core))
+    n_h = [bits(topo.mask(h, core)) for h in helpers_of(succ, core, T, topo)[0]]
+    one = 1 << topo.engines(core, succ)[0]
+
+    Qs = {"v": g.vector, "a": g.scalar, "p": g.tensor, "g": g, "s": g.sync}
+    csem = {"v": "cv", "a": "ca", "p": "cp", "g": "cg"}
+    total, waited, recs, bank = {}, {e: {} for e in Qs}, {}, {}
+
+    def need(e, who, reads, writes):
+        toks = []
+        for (b, lo, hi) in reads:
+            toks += [r[3] for r in recs.get(b, []) if r[2] == "w" and r[0] < hi and lo < r[1] and not (who == "p" and r[4] == "p")]
+        for (b, lo, hi) in writes:
+            toks += [r[3] for r in recs.get(b, []) if r[0] < hi and lo < r[1] and not (who == "p" and r[4] == "p")]
+        for (b, lo, hi) in reads + writes:
+            if SCRATCH[b][0] == "psum":
+                toks += [tk for w, tk in bank.get(b, {}).items() if w != who]
+        best = {}
+        for s, v in toks:
+            best[s] = max(best.get(s, 0), v)
+        for s, v in best.items():
+            wait(e, (s, v))
+
+    def wait(e, tok):
+        if waited[e].get(tok[0], 0) < tok[1]:
+            Qs[e].wait_ge(T.sem[tok[0]], tok[1])
+            waited[e][tok[0]] = tok[1]
+
+    def note(who, tok, reads, writes):
+        for (b, lo, hi) in writes:
+            recs[b] = [r for r in recs.get(b, []) if not (lo <= r[0] and r[1] <= hi)] + [(lo, hi, "w", tok, who)]
+        for (b, lo, hi) in reads:
+            recs[b] = [r for r in recs.get(b, []) if not (r[2] == "r" and r[4] == who and lo <= r[0] and r[1] <= hi)] + [(lo, hi, "r", tok, who)]
+        for (b, lo, hi) in reads + writes:
+            if SCRATCH[b][0] == "psum":
+                bank.setdefault(b, {})[who] = tok
+
+    def bump(s, k):
+        total[s] = total.get(s, 0) + k
+        return (s, total[s])
+
+    def op(e, fn, reads, writes):
+        need(e, e, reads, writes)
+        fn().then_inc(T.sem[csem[e]], 1)
+        note(e, bump(csem[e], 1), reads, writes)
+
+    def dma(items, sem, reads, writes):
+        who = "dma_" + sem + str(total.get(sem, 0))
+        for e in sorted(set(i[0] for i in items)):
+            need(e, who, reads, writes)
+        for e, o, i in items:
+            Qs[e].dma_start(o, i).then_inc(T.sem[sem], 16)
+        note(who, bump(sem, 16 * len(items)), reads, writes)
+
+    def arrival(sem, k, writes):
+        note("arr_" + sem, bump(sem, k), [], writes)
+
+    def c(b, lo=0, hi=None):
+        return (b, lo, SCRATCH[b][1][1] if hi is None else hi)
+
+    def ap(r):
+        return T[r[0]][:, r[1]:r[2]]
+
+    def ind(tab, lst):
+        return T[tab][:, 0:V].indirect(ap(lst))
+
+    vec, act, pe_ = g.vector, g.scalar, g.tensor
+
+    def tt(o, a, b, f):
+        op("v", lambda: vec.tensor_tensor(ap(o), ap(a), ap(b), f), [a, b], [o])
+
+    def ts(o, a, s1, s2, f0, f1=None, extra=()):
+        if f1 is None:
+            op("v", lambda: vec.tensor_scalar(ap(o), ap(a), s1, None, f0), [a] + list(extra), [o])
+        else:
+            op("v", lambda: vec.tensor_scalar(ap(o), ap(a), s1, s2, f0, f1), [a] + list(extra), [o])
+
+    def cp(o, a):
+        op("v", lambda: vec.tensor_copy(ap(o), ap(a)), [a], [o])
+
+    def av(o, a, f, bias=0.0, scale=1.0):
+        op("a", lambda: act.activation(ap(o), ap(a), f, bias=bias, scale=scale), [a], [o])
+
+    def gather(e, o, tab, lst):
+        if e == "v":
+            op("v", lambda: vec.tensor_copy(ap(o), ind(tab, lst)), [c(tab), lst], [o])
+        else:
+            op("a", lambda: act.activation(ap(o), ind(tab, lst), CPY), [c(tab), lst], [o])
+
+    def gather2(o, tab, lst):
+        h, k = (o[2] - o[1]) // 2, (lst[2] - lst[1]) // 2
+        gather("v", (o[0], o[1], o[1] + h), tab, (lst[0], lst[1], lst[1] + k))
+        gather("a", (o[0], o[1] + h, o[2]), tab, (lst[0], lst[1] + k, lst[2]))
+
+    def gsub(o, tab, lst, b):
+        op("v", lambda: vec.tensor_tensor(ap(o), ind(tab, lst), ap(b), SUB), [c(tab), lst, b], [o])
+
+    def mm(items, reads, writes):
+        def fn():
+            last = None
+            for o, l, r, st, sp in items:
+                last = pe_.matmul(o, l, r, st, sp)
+            return last
+        op("p", fn, reads, writes)
+
+    def wrap(src, width, sel, rot, b, dst, lo=0):
+        k = width // 16
+        items = []
+        for a in range(16):
+            s = (15 - a - 16 * rot) % 128
+            items.append((T[b][:, 0:k], T[sel][:, s:s + 128], T[src][:, lo + a:lo + width:16], a == 0, a == 15))
+        mm(items, [c(src, lo, lo + width), c(sel)], [c(b, 0, k)])
+        return lambda: cp(dst, c(b, 0, k))
+
+    def L(t, lo=0, hi=LR):
+        return (t * LR + lo, t * LR + hi)
+
+    def lst(i, lo=0, hi=LR):
+        return c("LS", 32 * i + lo // 16, 32 * i + hi // 16)
+
+    def gv(i, lo=0, hi=LR):
+        return c("GV", i * LR + lo, i * LR + hi)
+    GX, FD1, FD0, FC3, SC3, FC2, SC2, FC1, SC1, SD0 = range(10)
+
+    def halves(b, j):
+        return [c(b, h * (V // 2) + j * CW, h * (V // 2) + (j + 1) * CW) for h in range(2)]
+
+    def load_s(j, q):
+        a, b = halves("S", j)
+        dma([("s", ap(a), T.sat[:, a[1]:a[2]]), (q, ap(b), T.sat[:, b[1]:b[2]])], "ls%d" % j, [], [a, b])
+    dma([("s", ap(c("EC", 256, 384)), T.ex[:])], "lex", [], [c("EC", 256, 384)])
+    dma([("a", ap(c("EC", 128, 256)), T.pt[:])], "lpt", [], [c("EC", 128, 256)])
+    for j in range(NCH // 2):
+        load_s(j, "a")
+    op("g", lambda: g.iota(ap(c("EC", 0, 128)), [[1, 128]], 0, 128), [], [c("EC", 0, 128)])
+    op("g", lambda: g.iota(ap(c("PI", 0, 1)), [[1, 1]], 0, 1), [], [c("PI", 0, 1)])
+    op("g", lambda: g.iota(ap(c("I0")), [[1, 256]], 241, -1), [], [c("I0")])
+    op("g", lambda: g.iota(ap(c("KC")), [[0, 32], [-2048, 16]], 30720, 0, allow_small_or_imprecise_dtypes=True), [], [c("KC")])
+    op("v", lambda: vec.memset(ap(c("XI")), 0.0), [], [c("XI")])
+    ts(c("EC", 0, 128), c("EC", 0, 128), 2047, None, AND)
+    ts(c("PI", 1, 2), c("PI", 0, 1), 15, None, AND)
+    cp(c("EF", 0, 128), c("EC", 0, 128))
+    cp(c("PF", 0, 1), c("PI", 1, 2))
+    cp(c("EH", 0, 128), c("EF", 0, 128))
+    ts(c("PI", 2, 3), c("PI", 1, 2), 1, None, SHR)
+    tt(c("EH", 384, 512), c("EF", 0, 128), c("EH", 0, 128), SUB)
+    ts(c("I1"), c("I0"), ap(c("PF", 0, 1)), None, ADD, extra=[c("PF", 0, 1)])
+    cp(c("EF", 128, 384), c("EC", 128, 384))
+    cp(c("EH", 128, 384), c("EF", 128, 384))
+    ts(c("PF", 4, 5), c("PI", 2, 3), 2.0, None, EQ)
+    tt(c("EH", 512, 768), c("EF", 128, 384), c("EH", 128, 384), SUB)
+    dma([("sa"[h], T.XI[2 * m + h:128:16, :], ap(c("EH", 384 * h + 128 * m, 384 * h + 128 * m + 128))) for m in range(3) for h in range(2)],
+        "xd", [c("EH")], [c("XI")])
+    for j in range(NCH // 2, NCH):
+        load_s(j, "s")
+    need("g", "rs", [c("EH", 128, 384)], [])
+    ts(c("I2"), c("I1"), 127, None, AND)
+    ts(c("PF", 1, 2), c("PI", 2, 3), 0.0, None, EQ)
+    ts(c("PF", 2, 3), c("PI", 2, 3), 1.0, None, EQ)
+    ts(c("W2"), c("I2"), 0.0, ap(c("PF", 4, 5)), EQ, MUL, extra=[c("PF", 4, 5)])
+    ts(c("W0"), c("I2"), 0.0, ap(c("PF", 1, 2)), EQ, MUL, extra=[c("PF", 1, 2)])
+    ts(c("W1"), c("I2"), 0.0, ap(c("PF", 2, 3)), EQ, MUL, extra=[c("PF", 2, 3)])
+    ts(c("VB"), c("I2"), 0.0, None, EQ)
+    ts(c("I3"), c("I0", 15, 191), 127, None, AND)
+
+    def send_s(j):
+        ab = halves("S", j)
+        need("g", "rs", ab, [])
+        g.remote_dma_fused([RemoteDMATransfer(dst_ids=[hid[h]], dma_engine_mask=hm[h], remote_sem=T.sem["hh%d" % j],
+                                              src=ap(ab[h]), dst=ap(ab[h])) for h in range(2)], local_sem=T.sem.lsi)
+        bump("lsi", bits(hm[0]) + bits(hm[1]))
+        arrival("ad%d" % j, n_h[0], [halves("SN", j)[0]])
+        arrival("ah%d" % j, n_h[1], [halves("SN", j)[1]])
+    for j in range(NCH // 2):
+        send_s(j)
+
+    def ftab(src, dst, r, b, keep, onv=False):
+        lo, hi = r[1], r[2]
+        av(c("M", keep + lo, keep + hi), c(src, lo, hi), SQ)
+        if onv:
+            ts(c(b, 0, hi - lo), c(src, lo, hi), -1.0, 1.5, MUL, ADD)
+        else:
+            av(c(b, 0, hi - lo), c(src, lo, hi), IDF, bias=1.5, scale=-1.0)
+        return lambda: tt(c(dst, lo, hi), c("M", keep + lo, keep + hi), c(b, 0, hi - lo), MUL)
+
+    def htab(t, b):
+        av(c("TB"), c("S", *L(t)), SQ, bias=1.0, scale=-1.0)
+        av(c(b), c("TB"), IDF, scale=0.5)
+        return lambda: tt(c("H", *L(t)), c("M", *L(t)), c(b), ADD)
+
+    fl = [ftab("S", "F", halves("S", j)[h], "B%d" % (2 * j + h), 0) for j in range(NCH // 2) for h in range(2)]
+    ts(c("PF", 3, 4), c("PF", 0, 1), 1.0, None, ADD)
+    ts(c("I2", 0, 128), c("I1", 15, 143), 4, None, SHR)
+    ts(c("RB"), c("I3"), 0.0, None, EQ)
+    ts(c("BO"), c("I2", 0, 128), 16.0, ap(c("PF", 3, 4)), EQ, MUL, extra=[c("PF", 3, 4)])
+    w = wrap("XI", LR, "W2", 0, "B6", c("EXW", 0, 32))
+    wr = wrap("XI", V - LR, "W2", 0, "B7", c("EXW", 32, 128), LR)
+    op("v", lambda: vec.memset(ap(c("RM")), 1.0), [], [c("RM")])
+    for i, s in enumerate((1.0, 32768.0, -32768.0)):
+        ts(c("IDB", 128 * i, 128 * i + 128), c("I3", 0, 128), 0.0, s, EQ, MUL)
+    op("v", lambda: vec.memset(T.KC[:, 15:LR:16], 524288.0), [], [c("KC")])
+    op("v", lambda: vec.memset(T.RM[:, 0:LR:16], 0.0), [c("RM")], [c("RM")])
+    for k in range(K):
+        ts(c("BS", 128 * k, 128 * k + 128), c("BO"), float(k + 1), None, EQ)
+    w()
+
+    def conv(t, which):
+        cp(c(which, *L(t)), c("NBI", *L(t)))
+
+    WR = ["B6", "B7", "B0", "B1"]
+    CR = ["B4", "B5", "B6", "B7", "B0", "B2"]
+
+    def wmm(t, k):
+        b = WR[k % 4]
+        mm([(ap(c(b)), ap(c("BS", 128 * k, 128 * k + 128)), ap(c("TR", *L(t))), True, True)],
+           [c("BS", 128 * k, 128 * k + 128), c("TR", *L(t))], [c(b)])
+
+    def c1(t):
+        return c("EXW", 32 * t, 32 * t + 32)
+
+    for t in range(R):
+        if t == 0:
+            gather2(c("G0"), "XI", c1(0))
+            w = wrap("G0", LR, "W2", 0, "B6", lst(0))
+            wr()
+            need("g", "rx", [c("EXW")], [])
+            g.remote_dma(ap(c("EXN")), ap(c("EXW")), T.sem.aex, T.sem.lsr, ppid, prid, pm)
+            bump("lsr", bits(pm))
+            arrival("aex", n_s, [c("EXN")])
+            for j in range(NCH // 2, NCH):
+                send_s(j)
+            note("rs", ("lsi", total["lsi"]), [c("S")], [])
+            op("g", lambda: g.iota(ap(c("Q")), [[1, V]], 0, 0, allow_small_or_imprecise_dtypes=True), [], [c("Q")])
+            wait("s", ("lsi", total["lsi"]))
+            dma([("s", ap(c("NBI", 0, LR)), T.nb[:, 0:LR])], "ln0", [], [c("NBI", 0, LR)])
+            dma([("s", ap(c("TR")), T.tr[:])], "ltr", [], [c("TR")])
+            dma([("s", ap(c("NBI", LR, V)), T.nb[:, LR:V])], "ln1", [], [c("NBI", LR, V)])
+            for f in fl:
+                f()
+            fl = [ftab("S", "F", r, "B%d" % (i + 4), 0) for i, r in enumerate(halves("S", 2))]
+            w()
+            gather2(c("G1"), "XI", lst(0))
+            w = wrap("G1", LR, "W2", 0, "B7", lst(1))
+            for f in fl:
+                f()
+            fl = [ftab("S", "F", r, "B%d" % i, 0) for i, r in enumerate(halves("S", 3))]
+            w()
+            gather2(c("G0"), "XI", lst(1))
+            w = wrap("G0", LR, "W1", 0, "B6", lst(2))
+            for f in fl:
+                f()
+            f = htab(1, "B4")
+            gather("v", gv(FC3), "F", lst(1))
+            w()
+            f()
+            gather2(c("XN"), "XI", c("EXN"))
+            gather2(c("G0"), "XN", lst(2))
+        else:
+            gather2(c("G0"), "XP", c1(t))
+            w = wrap("G0", LR, "W0", 0, "B6", lst(0))
+            conv(t, "NBF")
+            w()
+            gather2(c("G1"), "XP", lst(0))
+            wd = wrap("G1", LR, "W1", t, "B7", lst(2))
+            wc = wrap("G1", LR, "W0", 0, "B6", lst(1))
+            gather2(gv(FC2), "F", lst(0))
+            gather2(c("XN", *L(t - 1)), "XI", c("NXN", 32 * (t - 1), 32 * t))
+            wd()
+            gather2(c("G0"), "XN", lst(2))
+            wc()
+        w = wrap("G0", LR, "W0", 0, "B7", lst(3))
+        if t == 0:
+            f = htab(2, "B2")
+            gather("v", gv(SC1), "S", c1(0))
+        else:
+            gather("v", gv(FD0), "FN", lst(2))
+            gather("a", c("FX", *L(t - 1)), "FN", c("NXN", 32 * (t - 1), 32 * t))
+        w()
+        gather2(c("G1"), "XN", lst(3))
+        w = wrap("G1", LR, "W0", 0, "B6", lst(4))
+        if t == 0:
+            f()
+            f = htab(3, "B3")
+        else:
+            gather("v", gv(FC3), "F", lst(1))
+            gather("a", gv(FD1), "FN", lst(3))
+        w()
+        if t == 0:
+            gather2(c("G0"), "XN", lst(4))
+            w = wrap("G0", LR, "W0", 0, "B7", lst(5))
+            f()
+            gather("a", gv(FC1), "F", c1(0))
+            gather("v", gv(FC2), "F", lst(0))
+            w()
+            pend = None
+            for j in range(NCH):
+                for h in range(2):
+                    f = ftab("SN", "FN", halves("SN", j)[h], "B%d" % ((2 * j + h) % 3), V, h == 1 and j % 2 == 0)
+                    if pend:
+                        pend()
+                    pend = f
+                if j in (1, 2):
+                    conv(0, ("NBU", "NBF")[j - 1])
+            pend()
+        wmm(t, 0)
+        wmm(t, 1)
+
+        tab1, l1 = ("FN", 5) if t == 0 else ("FX", 4)
+        for e, (lo, hi) in zip("aav", CH):
+            gather(e, gv(GX, lo, hi), tab1, lst(l1, lo, hi))
+        extra = {2: (SD0, "SN", 2), 3: (SC3, "S", 1), 4: (SC2, "S", 0)}
+        if t == 0:
+            gather("v", gv(FD1), "FN", lst(3))
+            gather("a", gv(FD0), "FN", lst(2))
+        fs = {2: FD1, 3: FD0, 4: FC3, 5: FC2, 6: FC1}
+        ss = {3: SD0, 4: SC3, 5: SC2, 6: SC1}
+        fused = {1: 4, 2: 3}
+        order = []
+        for s in range(1, 9):
+            for i in range(3):
+                for j in range(3):
+                    if not (s == 1 and j == 0) and not (s == 8 and j == 2):
+                        order.append((9 * s + 3 * i + 2 * j, s, i, j))
+        for _, s, i, j in sorted(order):
+            lo, hi = CH[i]
+            b = c("B%d" % i, 0, hi - lo)
+            y = c("S", *L(t, lo, hi)) if s == 7 else c("Y", lo, hi)
+            if s == 8:
+                if j == 0:
+                    if t < R - 1:
+                        ts(c("B4", lo, hi), c("S", *L(t, lo, hi)), -1.0, 1.5, MUL, ADD)
+                else:
+                    tt(c("H", *L(t, lo, hi)), c("TA", lo, hi), b, ADD)
+                continue
+            if j == 0:
+                tt(b, b, c("TB", lo, hi), MUL)
+            elif j == 1:
+                if s == 1:
+                    gsub(c("TD", lo, hi), "FN", lst(4, lo, hi), gv(GX, lo, hi))
+                elif s in fused:
+                    tt(c("TD", lo, hi), gv(fs[s], lo, hi), b, SUB)
+                else:
+                    tt(b, b, gv(fs[s], lo, hi) if s < 7 else c("F", *L(t, lo, hi)), SUB)
+            else:
+                if s in fused:
+                    gsub(y, "SN", lst(fused[s], lo, hi), c("TD", lo, hi))
+                else:
+                    tt(y, b, gv(ss[s], lo, hi) if s < 7 else y, ADD)
+                if s == 3 and t > 0:
+                    rb = c("B%d" % (3 + i), 0, hi - lo)
+                    mm([(ap(rb), T.RB[:, 16 * t:16 * t + 128], ap(y), True, True)], [c("RB"), y], [rb])
+                    y = rb
+                if s < 7:
+                    av(b, y, SQ)
+                    av(c("TB", lo, hi), y, IDF, bias=1.5, scale=-1.0)
+                    if s + 1 in extra:
+                        o, tab, li = extra[s + 1]
+                        gather("a", gv(o, lo, hi), tab, lst(li, lo, hi))
+                else:
+                    av(c("TB", lo, hi), y, SQ, bias=1.0, scale=-1.0)
+                    av(c("TA", lo, hi), y, SQ)
+                    av(b, c("TB", lo, hi), IDF, scale=0.5)
+                if s == 3 and i == 2:
+                    if t < R - 1:
+                        need("g", "rc", [], [c("SN"), c("FN")])
+                        g.remote_sem_update(T.sem["cr%d" % t], T.sem.lsr, spid, srid, one)
+                        bump("lsr", 1)
+                    items = [(ap(c("B3")), ap(c("IDB", 0, 128)), ap(c("KC")), True, False)]
+                    for k in range(K):
+                        items.append((T.B3[:, k:LR:16], T.RB[:, 0:128], ap(c("NBF", t * LR + 32 * k, t * LR + 32 * k + 32)), False, False))
+                    mm(items, [c("IDB"), c("KC"), c("RB"), c("NBF", *L(t))], [c("B3")])
+        dma([("s", T.ys[:, t * LR:(t + 1) * LR], ap(c("S", *L(t))))], "outs", [c("S", *L(t))], [])
+
+        def ug(k):
+            gather("a", c("U", (k % URING) * LR, (k % URING + 1) * LR), "H", c("NBU", t * LR + 32 * k, t * LR + 32 * k + 32))
+
+        def mk(k):
+            return c("M", k * LR, (k + 1) * LR)
+        gather2(c("U", 0, LR), "H", c("NBU", t * LR, t * LR + 32))
+        if t < R - 1:
+            tt(c("F", *L(t)), c("TA"), c("B4"), MUL)
+            g.wait_ge(T.sem["cr%d" % t], 1)
+            waited["g"]["cr%d" % t] = 1
+            bump("cr%d" % t, 1)
+            need("g", "rf", [c("S", *L(t)), c("F", *L(t))], [])
+            g.remote_dma_fused([
+                RemoteDMATransfer(dst_ids=[DstId(rid=prid, pnc=ppid)], dma_engine_mask=pm_a, remote_sem=T.sem["sf%d" % t],
+                                  src=ap(c("S", *L(t))), dst=ap(c("SN", *L(t)))),
+                RemoteDMATransfer(dst_ids=[DstId(rid=prid, pnc=ppid)], dma_engine_mask=pm_b, remote_sem=T.sem["sf%d" % t],
+                                  src=ap(c("F", *L(t))), dst=ap(c("FN", *L(t))))], local_sem=T.sem.lsr)
+            bump("lsr", bits(pm))
+            arrival("sf%d" % t, n_s, [c("SN", *L(t)), c("FN", *L(t))])
+        wmm(t, 2)
+        wmm(t, 3)
+        for k in range(1, URING):
+            ug(k)
+        for k in range(K + 1):
+            if k < K:
+                b = c(WR[k % 4])
+                tt(mk(0) if k == 0 else b, c("U", (k % URING) * LR, (k % URING + 1) * LR), b, MUL)
+                if k + URING < K:
+                    ug(k + URING)
+                if k == 0:
+                    wmm(t, 4)
+            if k >= 2:
+                b = c(WR[(k - 1) % 4])
+                tt(mk(k - 1) if k - 1 < 15 else b, mk(k - 2), b, MAX)
+                if k + 3 < K:
+                    wmm(t, k + 3)
+        mf = c(WR[15 % 4])
+        idle = []
+        if t < R - 1:
+            gather("a", gv(FC1), "F", c1(t + 1))
+            gather("a", gv(SC1), "S", c1(t + 1))
+            if t == 0:
+                idle += [(c("XP", *L(u)), "XI", c1(u)) for u in range(1, R)]
+            for u in range(R):
+                if u != t:
+                    idle.append((c("FX", *L(u)), "FN", c("NXN" if u < t else "EXN", 32 * u, 32 * u + 32)))
+        else:
+            for u in range(t):
+                gather("a", c("XO", *L(u)), "Q", c("NXO", 32 * u, 32 * u + 32))
+            dma([("s", T.yx[:, 0:t * LR], T.XO[0:128:16, 0:t * LR])], "outs", [c("XO", 0, t * LR)], [])
+        groups = [(k, min(k + 2, 15)) for k in range(0, 15, 2)]
+
+        def vupd(k0, k1):
+            items = []
+            for k in range(k0, k1):
+                items.append((T.B3[:, k:LR:16], ap(c("IDB", 128, 256)), ap(c("CS", 32 * k, 32 * k + 32)), False, False))
+                items.append((T.B3[:, k + 1:LR:16], ap(c("IDB", 256, 384)), ap(c("CS", 32 * k, 32 * k + 32)), False, k == 14))
+            mm(items, [c("IDB"), c("CS", 32 * k0, 32 * k1)], [c("B3")])
+        for j, (k0, k1) in enumerate(groups):
+            for k in range(k0, k1):
+                tt(c("Z", k * LR, (k + 1) * LR), mk(k), mf, GE)
+            cb = c(CR[j % 6], 32 * k0, 32 * k1)
+            mm([(ap(cb), T.VB[:, 15 - a:143 - a], T.Z[:, k0 * LR + a:k1 * LR:16], a == 0, a == 15) for a in range(16)],
+               [c("VB"), c("Z", k0 * LR, k1 * LR)], [cb])
+            if j > 0:
+                vupd(*groups[j - 1])
+            if idle:
+                gather("a", *idle.pop(0))
+            av(c("CS", 32 * k0, 32 * k1), cb, CPY)
+        vupd(*groups[-1])
+        if t < R - 1:
+            conv(t + 1, "NBU")
+        op("v", lambda: vec.tensor_tensor_scan(ap(c("BM")), ap(c("RM")), ap(c("B3")), 0.0, MUL, MAX), [c("RM"), c("B3")], [c("BM")])
+        op("v", lambda: vec.tensor_copy(ap(c("XA")), T.BM[:, 15:LR:16]), [c("BM")], [c("XA")])
+        ts(c("XB"), c("XA"), 2047, None, AND)
+        nx = c("NXO", 32 * t, 32 * t + 32)
+        cp(nx, c("XB"))
+        if t < R - 1:
+            need("g", "rn", [nx], [])
+            g.remote_dma(ap(c("NXN", nx[1], nx[2])), ap(nx), T.sem["nx%d" % t], T.sem.lsr, ppid, prid, pm)
+            bump("lsr", bits(pm))
+            arrival("nx%d" % t, n_s, [c("NXN", nx[1], nx[2])])
+            gather2(c("XP", *L(t)), "XI", nx)
+        else:
+            gather2(c("XO", *L(t)), "Q", nx)
+            dma([("s", T.yx[:, t * LR:V], T.XO[0:128:16, t * LR:V])], "outs", [c("XO", *L(t))], [])
+
+    for s in sorted(total):
+        wait("g", (s, total[s]))

@@ -2,43 +2,46 @@ from concourse.bass import DstId, RemoteDMATransfer
 from concourse.mybir import AluOpType, ActivationFunctionType
 
 V, K, R, LR = 2048, 16, 4, 512
-NCH = 4
+NCH = 2
 CW = V // (2 * NCH)
 URING = 6
-CH = [(0, 192), (192, 352), (352, 512)]
+CH = [(0, 128), (128, 256), (256, 384), (384, 512)]
 F32, BF, I32, U16 = "float32", "bfloat16", "int32", "uint16"
 
 SCRATCH = {}
-for _n in ("S", "F", "H", "SN", "FN", "FX", "Q", "XO", "NBF"):
+for _n in ("S", "NF", "H", "SN", "NFN", "FX", "Q", "XO", "NBF"):
     SCRATCH[_n] = ("sbuf", [128, V], F32)
+for _n in ("XI", "XP", "XN", "CL", "TR", "BS"):
+    SCRATCH[_n] = ("sbuf", [128, V], BF)
+for _n in ("Y", "GX", "TA", "TB", "TD", "BM"):
+    SCRATCH[_n] = ("sbuf", [128, LR], F32)
+for _n in ("G0", "G1", "EH", "EHN", "SP", "KC", "RM", "CS", "IDB"):
+    SCRATCH[_n] = ("sbuf", [128, LR], BF)
+for _n in ("EXW", "EXN", "NXO", "NXN"):
+    SCRATCH[_n] = ("sbuf", [128, 128], U16)
 SCRATCH.update({
-    "XI": ("sbuf", [128, V], BF), "NBI": ("sbuf", [128, V], I32), "NBU": ("sbuf", [128, V], U16),
-    "TR": ("sbuf", [128, V], BF), "U": ("sbuf", [128, URING * LR], F32), "M": ("sbuf", [128, 15 * LR], F32),
-    "Z": ("sbuf", [128, 15 * LR], BF), "GV": ("sbuf", [128, 10 * LR], F32), "XN": ("sbuf", [128, V], BF), "Y": ("sbuf", [128, LR], F32),
-    "TB": ("sbuf", [128, LR], F32), "TD": ("sbuf", [128, LR], F32), "TA": ("sbuf", [128, LR], F32),
-    "G0": ("sbuf", [128, LR], BF), "G1": ("sbuf", [128, LR], BF), "LS": ("sbuf", [128, 6 * 32], U16),
-    "EXW": ("sbuf", [128, 128], U16), "EXN": ("sbuf", [128, 128], U16), "NXO": ("sbuf", [128, 128], U16),
-    "NXN": ("sbuf", [128, 128], U16), "EC": ("sbuf", [128, 384], I32), "EF": ("sbuf", [128, 384], F32),
-    "EH": ("sbuf", [128, 768], BF), "XP": ("sbuf", [128, V], BF),
-    "W2": ("sbuf", [128, 256], BF), "I0": ("sbuf", [128, 256], I32), "I1": ("sbuf", [128, 256], I32),
-    "I2": ("sbuf", [128, 256], I32), "I3": ("sbuf", [128, 176], I32), "PI": ("sbuf", [128, 8], I32),
-    "PF": ("sbuf", [128, 8], F32), "VB": ("sbuf", [128, 256], BF), "W0": ("sbuf", [128, 256], BF),
-    "W1": ("sbuf", [128, 256], BF), "RB": ("sbuf", [128, 176], F32), "IDB": ("sbuf", [128, 384], BF),
-    "BO": ("sbuf", [128, 128], BF), "BS": ("sbuf", [128, 16 * 128], BF), "KC": ("sbuf", [128, LR], BF),
-    "RM": ("sbuf", [128, LR], BF), "CS": ("sbuf", [128, LR], BF), "BM": ("sbuf", [128, LR], F32),
-    "XA": ("sbuf", [128, 32], I32), "XB": ("sbuf", [128, 32], I32),
+    "NBI": ("sbuf", [128, V], I32), "NBU": ("sbuf", [128, V], U16),
+    "U": ("sbuf", [128, URING * LR], F32), "M": ("sbuf", [128, 15 * LR], F32), "Z": ("sbuf", [128, 15 * LR], BF),
+    "D1": ("sbuf", [128, 6 * 3 * LR], F32), "O": ("sbuf", [128, 3 * LR], F32),
+    "LS": ("sbuf", [128, 6 * 32], U16), "EC": ("sbuf", [128, LR], I32), "WS": ("sbuf", [128, 768], BF),
+    "I0": ("sbuf", [128, 176], I32), "I1": ("sbuf", [128, 80], I32), "RB": ("sbuf", [128, 176], F32),
+    "RBN": ("sbuf", [128, 128], F32), "CP": ("sbuf", [128, 384], BF), "C15": ("sbuf", [128, 256], BF), "XA": ("sbuf", [128, 32], I32), "XB": ("sbuf", [128, 32], I32),
 })
 for _b in range(8):
     SCRATCH["B%d" % _b] = ("psum", [128, 512], F32)
 
-SEMAPHORES = (["cv", "ca", "cp", "cg", "lex", "lpt", "xd", "ln0", "ln1", "ltr", "outs", "lsi", "lsr",
-               "aex"] + ["ls%d" % j for j in range(NCH)] + ["ad%d" % j for j in range(NCH)]
-              + ["ah%d" % j for j in range(NCH)] + ["hh%d" % j for j in range(NCH)]
-              + ["sf%d" % t for t in range(3)] + ["nx%d" % t for t in range(3)] + ["cr%d" % t for t in range(3)])
+NDMA = 48
+SEMAPHORES = (["cv", "ca", "cp", "cg", "lsi", "lsr", "aeh"] + ["d%d" % j for j in range(NDMA)]
+              + [s + str(j) for s in ("ad", "ah", "hh") for j in range(4)]
+              + [s + str(t) for s in ("sf", "nx", "cr") for t in range(R - 1)])
 
 ADD, SUB, MUL, MAX = AluOpType.add, AluOpType.subtract, AluOpType.mult, AluOpType.max
 AND, SHR, EQ, GE = AluOpType.bitwise_and, AluOpType.arith_shift_right, AluOpType.is_equal, AluOpType.is_ge
 SQ, IDF, CPY = ActivationFunctionType.Square, ActivationFunctionType.Identity, ActivationFunctionType.Copy
+
+CYC, PEC, GAT, HOP = 0.83e-3, 0.62e-3, 1.56, 0.1
+OPT = dict(first=10.0, step=1.5, pp=2, fb=40, q2="a", on={}, nx=2.6, peb=[(s, i) for s in (1, 2) for i in range(4)], u0=1, nf=2, seed=1, amp=1.5, win=5.0, fpe=0, npe=0)
+PLAN = []
 
 
 def bits(m):
@@ -60,6 +63,84 @@ def helper_program(g, core, half, n_in, dst, T, topo):
         g.wait_ge(T.sem["hh%d" % j], n_in)
         g.remote_dma(T.SN[:, lo:lo + CW], T.S[:, lo:lo + CW], T.sem[("ad%d", "ah%d")[half] % j], T.sem.lsi, pid, rid, m)
     g.wait_ge(T.sem.lsi, NCH * bits(m))
+
+
+def lay_out(ops):
+    for o in ops:
+        o["rest"] = o["lat"]
+    for o in reversed(ops):
+        o["rank"] = min(c for _, c, _ in o["opts"]) + o["rest"]
+        for d in o["deps"]:
+            ops[d]["rest"] = max(ops[d]["rest"], ops[d]["lat"] + HOP + o["rank"])
+        for d in o["behind"]:
+            ops[d]["rest"] = max(ops[d]["rest"], o["rank"])
+
+    def place(busy, e, t, c):
+        for s, f in busy.setdefault(e, []) if e != "x" else []:
+            if s >= t + c - 1e-9:
+                break
+            t = max(t, f)
+        return t
+
+    def take(busy, e, t, c):
+        if e != "x":
+            busy[e].append((t, t + c))
+            busy[e].sort()
+
+    def hop(a, b):
+        return 0 if a == b == "p" else HOP
+
+    def forward():
+        busy = {}
+        for o in sorted(ops, key=lambda o: (-round(o["rank"], 6), o["id"])):
+            best = None
+            for e, c, fn in o["opts"]:
+                t = place(busy, e, max([ops[d]["end"] + hop(e, ops[d]["eng"]) for d in o["deps"]]
+                                       + [ops[d]["end"] - ops[d]["lat"] for d in o["behind"]] + [0]), c)
+                if best is None or t + c < best[0] - 1e-9:
+                    best = (t + c, t, e, fn, c)
+            o["start"], o["eng"], o["fn"], o["cost"], o["end"] = best[1], best[2], best[3], best[4], best[0] + o["lat"]
+            take(busy, o["eng"], o["start"], o["cost"])
+        return max(o["end"] for o in ops)
+
+    def backward():
+        busy = {}
+        for o in ops:
+            o["rest"] = o["lat"]
+        for o in sorted(ops, key=lambda o: (-round(o["start"] + o["cost"], 6), -o["id"])):
+            t = place(busy, o["eng"], o["rest"], o["cost"])
+            take(busy, o["eng"], t, o["cost"])
+            o["rank"] = t + o["cost"]
+            for d in o["deps"]:
+                ops[d]["rest"] = max(ops[d]["rest"], ops[d]["lat"] + hop(o["eng"], ops[d]["eng"]) + o["rank"])
+            for d in o["behind"]:
+                ops[d]["rest"] = max(ops[d]["rest"], o["rank"])
+
+    if not PLAN:
+        best, seed = None, OPT["seed"]
+        for n in range(OPT["fb"] + 1):
+            span = forward()
+            if best is None or span < best[0]:
+                best = (span, [(o["start"], o["eng"]) for o in ops], [(o["cost"], o["end"]) for o in ops])
+            if n % 2:
+                for o, (s, e), (c, f) in zip(ops, best[1], best[2]):
+                    o["start"], o["eng"], o["cost"], o["end"] = s, e, c, f
+            backward()
+            if n % 2:
+                seed = (seed * 1103515245 + 12345) % 2147483648
+                t0 = best[0] * seed / 2147483648
+                for o in reversed(ops):
+                    seed = (seed * 1103515245 + 12345) % 2147483648
+                    o["rank"] = max(o["rank"] + (OPT["amp"] * (seed / 2147483648 - 0.5) if t0 < o["start"] < t0 + OPT["win"] else 0), o.get("floor", 0))
+                    for d in o["deps"] + o["behind"]:
+                        ops[d]["floor"] = max(ops[d].get("floor", 0), o["rank"] + 1e-3)
+                for o in ops:
+                    o["floor"] = 0
+        PLAN.extend(best[1])
+        OPT["span"] = best[0]
+    for o, (s, e) in zip(ops, PLAN):
+        o["start"], o["eng"], o["fn"] = s, e, [fn for q, _, fn in o["opts"] if q == e][0]
+    return sorted(ops, key=lambda o: (o["start"], o["id"]))
 
 
 def rank_program(g, core, T, topo):
@@ -84,462 +165,434 @@ def rank_program(g, core, T, topo):
     n_s = bits(topo.mask(succ, core))
     n_h = [bits(topo.mask(h, core)) for h in helpers_of(succ, core, T, topo)[0]]
     one = 1 << topo.engines(core, succ)[0]
+    vec, act, pe_ = g.vector, g.scalar, g.tensor
+    Qs = {"v": vec, "a": act, "p": pe_, "g": g, "s": g.sync}
 
-    Qs = {"v": g.vector, "a": g.scalar, "p": g.tensor, "g": g, "s": g.sync}
-    csem = {"v": "cv", "a": "ca", "p": "cp", "g": "cg"}
-    total, waited, recs, bank = {}, {e: {} for e in Qs}, {}, {}
+    ops, recs, bank, total, ndma = [], {}, {}, {}, [0]
+    hint = []
 
-    def need(e, who, reads, writes):
-        toks = []
+    def psum(r):
+        return r[0][0] == "B" and r[0][1:].isdigit()
+
+    def add(opts, reads, writes, lat=0.0, tok="own", after=(), record=True):
+        i = len(ops)
+        behind = list(hint)
+        del hint[:]
+        deps = set(after)
         for (b, lo, hi) in reads:
-            toks += [r[3] for r in recs.get(b, []) if r[2] == "w" and r[0] < hi and lo < r[1] and not (who == "p" and r[4] == "p")]
+            deps |= {r[3] for r in recs.get(b, []) if r[2] == "w" and r[0] < hi and lo < r[1]}
         for (b, lo, hi) in writes:
-            toks += [r[3] for r in recs.get(b, []) if r[0] < hi and lo < r[1] and not (who == "p" and r[4] == "p")]
-        for (b, lo, hi) in reads + writes:
-            if SCRATCH[b][0] == "psum":
-                toks += [tk for w, tk in bank.get(b, {}).items() if w != who]
-        best = {}
-        for s, v in toks:
-            best[s] = max(best.get(s, 0), v)
-        for s, v in best.items():
-            wait(e, (s, v))
-
-    def wait(e, tok):
-        if waited[e].get(tok[0], 0) < tok[1]:
-            Qs[e].wait_ge(T.sem[tok[0]], tok[1])
-            waited[e][tok[0]] = tok[1]
-
-    def note(who, tok, reads, writes):
-        for (b, lo, hi) in writes:
-            recs[b] = [r for r in recs.get(b, []) if not (lo <= r[0] and r[1] <= hi)] + [(lo, hi, "w", tok, who)]
-        for (b, lo, hi) in reads:
-            recs[b] = [r for r in recs.get(b, []) if not (r[2] == "r" and r[4] == who and lo <= r[0] and r[1] <= hi)] + [(lo, hi, "r", tok, who)]
-        for (b, lo, hi) in reads + writes:
-            if SCRATCH[b][0] == "psum":
-                bank.setdefault(b, {})[who] = tok
+            deps |= {r[3] for r in recs.get(b, []) if r[0] < hi and lo < r[1]}
+        who = opts[0][0] if len(opts) == 1 else i
+        for b in {r[0] for r in reads + writes if psum(r)}:
+            w, cur, old = bank.get(b, (None, [], []))
+            if w == who:
+                deps |= set(old)
+                cur.append(i)
+            else:
+                deps |= set(cur)
+                bank[b] = (who, [i], cur)
+        if record:
+            for (b, lo, hi) in writes:
+                recs[b] = [r for r in recs.get(b, []) if not (lo <= r[0] and r[1] <= hi)] + [(lo, hi, "w", i)]
+            for (b, lo, hi) in reads:
+                recs.setdefault(b, []).append((lo, hi, "r", i))
+        ops.append({"id": i, "opts": opts, "deps": sorted(deps), "behind": behind, "lat": lat, "tok": tok})
+        return i
 
     def bump(s, k):
         total[s] = total.get(s, 0) + k
         return (s, total[s])
 
-    def op(e, fn, reads, writes):
-        need(e, e, reads, writes)
-        fn().then_inc(T.sem[csem[e]], 1)
-        note(e, bump(csem[e], 1), reads, writes)
+    def dma(e, o, i, reads, writes, lat=2.5, after=(), **kw):
+        s = "d%d" % ndma[0]
+        ndma[0] += 1
+        return add([(e, 0.6 if e == "g" else 0.05, lambda: Qs[e].dma_start(o, i, **kw).then_inc(T.sem[s], 16))], reads, writes, lat, bump(s, 16), after)
 
-    def dma(items, sem, reads, writes):
-        who = "dma_" + sem + str(total.get(sem, 0))
-        for e in sorted(set(i[0] for i in items)):
-            need(e, who, reads, writes)
-        for e, o, i in items:
-            Qs[e].dma_start(o, i).then_inc(T.sem[sem], 16)
-        note(who, bump(sem, 16 * len(items)), reads, writes)
+    def remote(fn, reads, after=(), cost=0.3):
+        return add([("g", cost, fn)], reads, [], 0.0, None, after, False)
 
-    def arrival(sem, k, writes):
-        note("arr_" + sem, bump(sem, k), [], writes)
+    def event(sem, k, lat, after, reads=(), writes=()):
+        return add([("x", lat, None)], list(reads), list(writes), 0.0, bump(sem, k), after)
 
     def c(b, lo=0, hi=None):
         return (b, lo, SCRATCH[b][1][1] if hi is None else hi)
 
+    def part(nm, j, s, lo=0, hi=LR):
+        return ("@%s.%d.%d" % (nm, j, s), lo, hi)
+
     def ap(r):
-        return T[r[0]][:, r[1]:r[2]]
+        b, lo, hi = r
+        if b[0] == "@":
+            nm, j, s = b[1:].split(".")
+            o = 3 * LR * int(s) + int(j)
+            return T[nm][:, o + 3 * lo:o + 3 * hi - 2:3]
+        return T[b][:, lo:hi]
 
-    def ind(tab, lst):
-        return T[tab][:, 0:V].indirect(ap(lst))
+    def w(r):
+        return r[2] - r[1]
 
-    vec, act, pe_ = g.vector, g.scalar, g.tensor
+    def cv(k):
+        return 0.03 + max(64, k) * CYC
+
+    def ca(k):
+        return 0.05 + max(64, k) * CYC
+
+    def vop(fn, k, reads, writes, **kw):
+        return add([("v", cv(k), fn)], reads, writes, **kw)
+
+    def gop(fn, k, reads, writes, **kw):
+        return add([("g", 0.14 + 2 * k * CYC, fn)], reads, writes, **kw)
 
     def tt(o, a, b, f):
-        op("v", lambda: vec.tensor_tensor(ap(o), ap(a), ap(b), f), [a, b], [o])
+        return vop(lambda: vec.tensor_tensor(ap(o), ap(a), ap(b), f), w(o) * (1 if psum(a) or psum(b) else 2), [a, b], [o])
 
-    def ts(o, a, s1, s2, f0, f1=None, extra=()):
-        if f1 is None:
-            op("v", lambda: vec.tensor_scalar(ap(o), ap(a), s1, None, f0), [a] + list(extra), [o])
-        else:
-            op("v", lambda: vec.tensor_scalar(ap(o), ap(a), s1, s2, f0, f1), [a] + list(extra), [o])
+    def ts(o, a, s1, f0, oap=None):
+        vop(lambda: vec.tensor_scalar(oap if oap is not None else ap(o), ap(a), s1, None, f0), w(a), [a], [o])
 
     def cp(o, a):
-        op("v", lambda: vec.tensor_copy(ap(o), ap(a)), [a], [o])
+        vop(lambda: vec.tensor_copy(ap(o), ap(a)), w(o), [a], [o])
 
-    def av(o, a, f, bias=0.0, scale=1.0):
-        op("a", lambda: act.activation(ap(o), ap(a), f, bias=bias, scale=scale), [a], [o])
+    def sq(o, a, bias=0.0, scale=1.0):
+        add([("a", ca(w(o)), lambda: act.activation(ap(o), ap(a), SQ, bias=bias, scale=scale))], [a], [o])
 
-    def gather(e, o, tab, lst):
-        if e == "v":
-            op("v", lambda: vec.tensor_copy(ap(o), ind(tab, lst)), [c(tab), lst], [o])
-        else:
-            op("a", lambda: act.activation(ap(o), ind(tab, lst), CPY), [c(tab), lst], [o])
+    def lin(o, a, scale, bias, on="av"):
+        opts = {"a": ("a", ca(w(o)), lambda: act.activation(ap(o), ap(a), IDF, bias=bias, scale=scale)),
+                "v": ("v", cv(w(o)), lambda: vec.tensor_scalar(ap(o), ap(a), scale, bias, MUL, ADD))}
+        add([opts[e] for e in on], [a], [o])
 
-    def gather2(o, tab, lst):
-        h, k = (o[2] - o[1]) // 2, (lst[2] - lst[1]) // 2
-        gather("v", (o[0], o[1], o[1] + h), tab, (lst[0], lst[1], lst[1] + k))
-        gather("a", (o[0], o[1] + h, o[2]), tab, (lst[0], lst[1] + k, lst[2]))
+    def ind(tab, ls):
+        return T[tab][:, 0:V].indirect(ap(ls))
 
-    def gsub(o, tab, lst, b):
-        op("v", lambda: vec.tensor_tensor(ap(o), ind(tab, lst), ap(b), SUB), [c(tab), lst, b], [o])
+    def gather(o, tab, ls, on="av", parts=1):
+        for p in range(parts):
+            h, k = w(o) // parts, w(ls) // parts
+            oo, ll = (o[0], o[1] + p * h, o[1] + (p + 1) * h), (ls[0], ls[1] + p * k, ls[1] + (p + 1) * k)
+            opts = {"a": ("a", 0.065 + h * GAT * CYC, lambda oo=oo, ll=ll: act.activation(ap(oo), ind(tab, ll), CPY)),
+                    "v": ("v", 0.05 + h * GAT * CYC, lambda oo=oo, ll=ll: vec.tensor_copy(ap(oo), ind(tab, ll)))}
+            add([opts[e] for e in on], [c(tab), ll], [oo])
 
-    def mm(items, reads, writes):
+    def gtt(o, tab, ls, b, f):
+        add([("v", 0.05 + w(o) * GAT * CYC, lambda: vec.tensor_tensor(ap(o), ind(tab, ls), ap(b), f))], [c(tab), ls, b], [o])
+
+    def mm(items, cyc, reads, writes):
         def fn():
             last = None
             for o, l, r, st, sp in items:
                 last = pe_.matmul(o, l, r, st, sp)
             return last
-        op("p", fn, reads, writes)
+        add([("p", cyc * PEC, fn)], reads, writes)
 
-    def wrap(src, width, sel, rot, b, dst, lo=0):
+    W0, W1, VB = 0, 256, 512
+
+    def wrap(src, lo, width, sel, rot, b, dst):
         k = width // 16
         items = []
         for a in range(16):
-            s = (15 - a - 16 * rot) % 128
-            items.append((T[b][:, 0:k], T[sel][:, s:s + 128], T[src][:, lo + a:lo + width:16], a == 0, a == 15))
-        mm(items, [c(src, lo, lo + width), c(sel)], [c(b, 0, k)])
-        return lambda: cp(dst, c(b, 0, k))
+            s = sel + (15 - a - 16 * rot) % 128
+            items.append((T[b][:, 0:k], T.WS[:, s:s + 128], T[src][:, lo + a:lo + width:16], a == 0, a == 15))
+        mm(items, 16 * max(64, k), [c(src, lo, lo + width), c("WS", sel, sel + 256)], [c(b, 0, k)])
+        cp(dst, c(b, 0, k))
 
     def L(t, lo=0, hi=LR):
         return (t * LR + lo, t * LR + hi)
 
     def lst(i, lo=0, hi=LR):
         return c("LS", 32 * i + lo // 16, 32 * i + hi // 16)
-
-    def gv(i, lo=0, hi=LR):
-        return c("GV", i * LR + lo, i * LR + hi)
-    GX, FD1, FD0, FC3, SC3, FC2, SC2, FC1, SC1, SD0 = range(10)
-
-    def halves(b, j):
-        return [c(b, h * (V // 2) + j * CW, h * (V // 2) + (j + 1) * CW) for h in range(2)]
-
-    def load_s(j, q):
-        a, b = halves("S", j)
-        dma([("s", ap(a), T.sat[:, a[1]:a[2]]), (q, ap(b), T.sat[:, b[1]:b[2]])], "ls%d" % j, [], [a, b])
-    dma([("s", ap(c("EC", 256, 384)), T.ex[:])], "lex", [], [c("EC", 256, 384)])
-    dma([("a", ap(c("EC", 128, 256)), T.pt[:])], "lpt", [], [c("EC", 128, 256)])
-    for j in range(NCH // 2):
-        load_s(j, "a")
-    op("g", lambda: g.iota(ap(c("EC", 0, 128)), [[1, 128]], 0, 128), [], [c("EC", 0, 128)])
-    op("g", lambda: g.iota(ap(c("PI", 0, 1)), [[1, 1]], 0, 1), [], [c("PI", 0, 1)])
-    op("g", lambda: g.iota(ap(c("I0")), [[1, 256]], 241, -1), [], [c("I0")])
-    op("g", lambda: g.iota(ap(c("KC")), [[0, 32], [-2048, 16]], 30720, 0, allow_small_or_imprecise_dtypes=True), [], [c("KC")])
-    op("v", lambda: vec.memset(ap(c("XI")), 0.0), [], [c("XI")])
-    ts(c("EC", 0, 128), c("EC", 0, 128), 2047, None, AND)
-    ts(c("PI", 1, 2), c("PI", 0, 1), 15, None, AND)
-    cp(c("EF", 0, 128), c("EC", 0, 128))
-    cp(c("PF", 0, 1), c("PI", 1, 2))
-    cp(c("EH", 0, 128), c("EF", 0, 128))
-    ts(c("PI", 2, 3), c("PI", 1, 2), 1, None, SHR)
-    tt(c("EH", 384, 512), c("EF", 0, 128), c("EH", 0, 128), SUB)
-    ts(c("I1"), c("I0"), ap(c("PF", 0, 1)), None, ADD, extra=[c("PF", 0, 1)])
-    cp(c("EF", 128, 384), c("EC", 128, 384))
-    cp(c("EH", 128, 384), c("EF", 128, 384))
-    ts(c("PF", 4, 5), c("PI", 2, 3), 2.0, None, EQ)
-    tt(c("EH", 512, 768), c("EF", 128, 384), c("EH", 128, 384), SUB)
-    dma([("sa"[h], T.XI[2 * m + h:128:16, :], ap(c("EH", 384 * h + 128 * m, 384 * h + 128 * m + 128))) for m in range(3) for h in range(2)],
-        "xd", [c("EH")], [c("XI")])
-    for j in range(NCH // 2, NCH):
-        load_s(j, "s")
-    need("g", "rs", [c("EH", 128, 384)], [])
-    ts(c("I2"), c("I1"), 127, None, AND)
-    ts(c("PF", 1, 2), c("PI", 2, 3), 0.0, None, EQ)
-    ts(c("PF", 2, 3), c("PI", 2, 3), 1.0, None, EQ)
-    ts(c("W2"), c("I2"), 0.0, ap(c("PF", 4, 5)), EQ, MUL, extra=[c("PF", 4, 5)])
-    ts(c("W0"), c("I2"), 0.0, ap(c("PF", 1, 2)), EQ, MUL, extra=[c("PF", 1, 2)])
-    ts(c("W1"), c("I2"), 0.0, ap(c("PF", 2, 3)), EQ, MUL, extra=[c("PF", 2, 3)])
-    ts(c("VB"), c("I2"), 0.0, None, EQ)
-    ts(c("I3"), c("I0", 15, 191), 127, None, AND)
-
-    def send_s(j):
-        ab = halves("S", j)
-        need("g", "rs", ab, [])
-        g.remote_dma_fused([RemoteDMATransfer(dst_ids=[hid[h]], dma_engine_mask=hm[h], remote_sem=T.sem["hh%d" % j],
-                                              src=ap(ab[h]), dst=ap(ab[h])) for h in range(2)], local_sem=T.sem.lsi)
-        bump("lsi", bits(hm[0]) + bits(hm[1]))
-        arrival("ad%d" % j, n_h[0], [halves("SN", j)[0]])
-        arrival("ah%d" % j, n_h[1], [halves("SN", j)[1]])
-    for j in range(NCH // 2):
-        send_s(j)
-
-    def ftab(src, dst, r, b, keep, onv=False):
-        lo, hi = r[1], r[2]
-        av(c("M", keep + lo, keep + hi), c(src, lo, hi), SQ)
-        if onv:
-            ts(c(b, 0, hi - lo), c(src, lo, hi), -1.0, 1.5, MUL, ADD)
-        else:
-            av(c(b, 0, hi - lo), c(src, lo, hi), IDF, bias=1.5, scale=-1.0)
-        return lambda: tt(c(dst, lo, hi), c("M", keep + lo, keep + hi), c(b, 0, hi - lo), MUL)
-
-    def htab(t, b):
-        av(c("TB"), c("S", *L(t)), SQ, bias=1.0, scale=-1.0)
-        av(c(b), c("TB"), IDF, scale=0.5)
-        return lambda: tt(c("H", *L(t)), c("M", *L(t)), c(b), ADD)
-
-    fl = [ftab("S", "F", halves("S", j)[h], "B%d" % (2 * j + h), 0) for j in range(NCH // 2) for h in range(2)]
-    ts(c("PF", 3, 4), c("PF", 0, 1), 1.0, None, ADD)
-    ts(c("I2", 0, 128), c("I1", 15, 143), 4, None, SHR)
-    ts(c("RB"), c("I3"), 0.0, None, EQ)
-    ts(c("BO"), c("I2", 0, 128), 16.0, ap(c("PF", 3, 4)), EQ, MUL, extra=[c("PF", 3, 4)])
-    w = wrap("XI", LR, "W2", 0, "B6", c("EXW", 0, 32))
-    wr = wrap("XI", V - LR, "W2", 0, "B7", c("EXW", 32, 128), LR)
-    op("v", lambda: vec.memset(ap(c("RM")), 1.0), [], [c("RM")])
-    for i, s in enumerate((1.0, 32768.0, -32768.0)):
-        ts(c("IDB", 128 * i, 128 * i + 128), c("I3", 0, 128), 0.0, s, EQ, MUL)
-    op("v", lambda: vec.memset(T.KC[:, 15:LR:16], 524288.0), [], [c("KC")])
-    op("v", lambda: vec.memset(T.RM[:, 0:LR:16], 0.0), [c("RM")], [c("RM")])
-    for k in range(K):
-        ts(c("BS", 128 * k, 128 * k + 128), c("BO"), float(k + 1), None, EQ)
-    w()
-
-    def conv(t, which):
-        cp(c(which, *L(t)), c("NBI", *L(t)))
-
-    WR = ["B6", "B7", "B0", "B1"]
-    CR = ["B4", "B5", "B6", "B7", "B0", "B2"]
-
-    def wmm(t, k):
-        b = WR[k % 4]
-        mm([(ap(c(b)), ap(c("BS", 128 * k, 128 * k + 128)), ap(c("TR", *L(t))), True, True)],
-           [c("BS", 128 * k, 128 * k + 128), c("TR", *L(t))], [c(b)])
+    C2, C3, D0, D1, D2, D3 = range(6)
 
     def c1(t):
         return c("EXW", 32 * t, 32 * t + 32)
 
+    def iota(o, pattern, base, cm, after=()):
+        kw = {} if o[0] in ("I0", "I1") else {"allow_small_or_imprecise_dtypes": True}
+        return gop(lambda: g.iota(ap(o), pattern, base, cm, **kw), w(o), [], [o], after=after)
+
+    def halves(b, j):
+        return [c(b, h * (V // 2) + j * CW, h * (V // 2) + (j + 1) * CW) for h in range(2)]
+
+    for q in range(4):
+        dma("sa"[q % 2], T.EC[32 * q:32 * q + 32, :], (T.ex, T.pt)[q % 2][:], [], [("EC%d" % q, 0, 1)], 2.0)
+    for j in range(NCH):
+        for h, r in enumerate(halves("S", j)):
+            hint.extend(range(len(ops)))
+            dma("s", ap(r), T.sat[:, r[1]:r[2]], [], [r], 2.4 + 2.0 / NCH * (2 * j + h + 1))
+    iota(c("I1", 0, 32), [[-1, 4], [-4, 8]], 0, 1)
+    iota(c("I1", 32, 48), [[0, 2], [-16, 8]], 0, 1)
+    iota(c("I0"), [[1, 176]], 0, -1)
+    vop(lambda: vec.memset(ap(c("SP")), 0.0), 256, [], [c("SP")])
+    vop(lambda: vec.memset(ap(c("WS")), 0.0), 384, [], [c("WS")])
+    for q in range(4):
+        ts(c("SP"), c("I1", 0, 32), float(32 * q), EQ, T.SP[:, (0, 2, 1, 3)[q]:LR:16])
+    ts(c("I1", 48, 64), c("I1", 32, 48), 1, SHR)
+    ts(c("I1", 64, 80), c("I1", 32, 48), 4, SHR)
+    ts(c("WS", W0, W0 + 256), c("I1", 48, 64), 0.0, EQ, T.WS[:, W0 + 15:W0 + 256:16])
+    ts(c("WS", W1, W1 + 256), c("I1", 48, 64), 1.0, EQ, T.WS[:, W1 + 15:W1 + 256:16])
+    ts(c("WS", VB, VB + 256), c("I1", 64, 80), 0.0, EQ, T.WS[:, VB + 15:VB + 256:16])
+    ecs = [("EC%d" % q, 0, 1) for q in range(4)]
+    vop(lambda: vec.tensor_scalar(T.EH[:, :], T.EC[:, :], 1.0, None, MUL), LR, ecs, [c("EH")])
+    vop(lambda: vec.tensor_tensor(T.EH[64:128, :], T.EC[64:128, :], T.EH[64:128, :], SUB), 2 * LR, ecs + [c("EH")], [c("EH")])
+
+    def spread(dst, src):
+        for a in range(4):
+            b = c("B%d" % a)
+            mm([(ap(b), T.SP[:, 128 * a:128 * a + 128], ap(c(src)), True, True)], LR, [c("SP"), c(src)], [b])
+            lin(c(dst, *L(a)), b, 1.0, 0.0)
+    spread("XP", "EH")
+    s_ = remote(lambda: g.remote_dma(ap(c("EHN")), ap(c("EH")), T.sem.aeh, T.sem.lsr, ppid, prid, pm), [c("EH")], cost=1.5)
+    bump("lsr", bits(pm))
+    event("aeh", n_s, 3.0, [s_], writes=[c("EHN")])
+    sends = []
+    for j in range(NCH):
+        ab = halves("S", j)
+        s_ = remote(lambda ab=ab, j=j: g.remote_dma_fused(
+            [RemoteDMATransfer(dst_ids=[hid[h]], dma_engine_mask=hm[h], remote_sem=T.sem["hh%d" % j], src=ap(ab[h]), dst=ap(ab[h]))
+             for h in range(2)], local_sem=T.sem.lsi), ab, after=[s_])
+        sends.append(s_)
+        for h in range(2):
+            event(("ad%d", "ah%d")[h] % j, n_h[h], OPT["first"] + j * OPT["step"], [s_], writes=[halves("SN", j)[h]])
+    left = event("lsi", NCH * (bits(hm[0]) + bits(hm[1])), 5.0, sends, reads=[c("S")])
+    wrap("XP", 0, LR, W0, 0, "B6", c1(0))
+
+    ts(c("RB", 0, 128), c("I0", 0, 128), 0.0, EQ)
+    ts(c("RB", 128, 176), c("I0", 128, 176), 128.0, EQ)
+    for i, s in enumerate((1.0, 32768.0, -32768.0, -1.0)):
+        lin(c("IDB", 128 * i, 128 * i + 128), c("RB", 0, 128), s, 0.0)
+    vop(lambda: vec.memset(ap(c("C15")), 1.5), 128, [], [c("C15")])
+
+    def ftab(src, dst, r, b, keep, pe=False):
+        lo, hi = r[1], r[2]
+        sq(c("M", keep + lo, keep + hi), c(src, lo, hi))
+        if pe:
+            for x in range(0, hi - lo, 256):
+                mm([(T[b][:, x:x + 256], T.IDB[:, 384:512], T.C15[:, :], True, False), (T[b][:, x:x + 256], T.RB[:, 0:128], T[src][:, lo + x:lo + x + 256], False, True)],
+                   5 * 256, [c("IDB"), c("C15"), c("RB"), c(src, lo, hi)], [c(b, x, x + 256)])
+        else:
+            lin(c(b, 0, hi - lo), c(src, lo, hi), 1.0, -1.5)
+        tt(c(dst, lo, hi), c("M", keep + lo, keep + hi), c(b, 0, hi - lo), MUL)
+
+    for i, u in enumerate((0, 2, 1, 3)):
+        ftab("S", "NF", c("S", *L(u)), "B%d" % (4 + i % 2), 0, i < OPT["fpe"])
+    lin(c("RBN"), c("RB", 0, 128), -1.0, 0.0)
+    for j, s in enumerate((0.0, 1.5, 1.0)):
+        vop(lambda j=j, s=s: vec.memset(T.CP[:, j:384:3], s), 64, [], [c("CP")])
+    iota(c("KC"), [[0, 32], [-2048, 16]], 30720, 0, after=sends)
+    vop(lambda: vec.memset(T.KC[:, 15:LR:16], 524288.0), 32, [], [c("KC")])
+    vop(lambda: vec.memset(ap(c("RM")), 1.0), 256, [], [c("RM")])
+    vop(lambda: vec.memset(T.RM[:, 0:LR:16], 0.0), 32, [], [c("RM")])
+    iota(c("BS"), [[0, V]], 1, 0, after=sends)
+    gop(lambda: g.affine_select(ap(c("BS")), ap(c("BS")), [[-1, 16], [-16, 8], [0, 16]], EQ, 0.0, 0, 1), V, [c("BS")], [c("BS")])
+    iota(c("XI"), [[16, 128], [0, 16]], 0, 0, after=sends)
+    iota(c("CL"), [[0, 128], [1, 16]], 0, 0, after=sends)
+    iota(c("Q"), [[1, V]], 0, 0, after=sends)
+    dma("s", ap(c("NBI", 0, LR)), T.nb[:, 0:LR], [], [c("NBI", 0, LR)], after=[left])
+    dma("s", ap(c("TR")), T.tr[:], [], [c("TR")], 4.0, after=[left])
+    dma("s", ap(c("NBI", LR, V)), T.nb[:, LR:V], [], [c("NBI", LR, V)], 6.0, after=[left])
+    xi = [dma("s", T.XI[1:128:16, :], T.CL[0:8, :], [c("CL"), c("XI")], [("XI1", 0, 1)])]
+    for r in (2, 3):
+        xi.append(dma("s", T.XI[r:128:16, :], T.XP[r:128:16, :], [c("XP"), c("XI")], [("XI%d" % r, 0, 1)]))
+    for i in xi:
+        recs["XI"].append((0, V, "w", i))
+
+    WR = ["B5", "B6", "B7", "B4"]
+    SB = ["B0", "B1", "B2", "B4"]
+    CR = ["B0", "B1", "B2"]
+
+    def pre(s, far, ls, on="av"):
+        a, b = OPT["on"].get(s, (on, on))
+        gather(part("D1", 1, s - 2), ("NF", "NFN")[far], ls, a, OPT["pp"])
+        gather(part("D1", 2, s - 2), ("S", "SN")[far], ls, b, OPT["pp"])
+
+    def own(t, on):
+        pre(6, 0, c1(t), on)
+        for j, a in ((1, c("NF", *L(t))), (2, c("S", *L(t)))):
+            gop(lambda j=j, a=a: g.affine_select(ap(part("D1", j, 5)), ap(a), [[0, LR]], GE, 0.0, 0, 0), LR, [a], [part("D1", j, 5)])
+
     for t in range(R):
+        gather(c("G0"), "XP", c1(t), parts=2)
+        wrap("G0", 0, LR, W0, 0, "B7", lst(C2))
+        gather(c("G1"), "XP", lst(C2), parts=2)
         if t == 0:
-            gather2(c("G0"), "XI", c1(0))
-            w = wrap("G0", LR, "W2", 0, "B6", lst(0))
-            wr()
-            need("g", "rx", [c("EXW")], [])
-            g.remote_dma(ap(c("EXN")), ap(c("EXW")), T.sem.aex, T.sem.lsr, ppid, prid, pm)
-            bump("lsr", bits(pm))
-            arrival("aex", n_s, [c("EXN")])
-            for j in range(NCH // 2, NCH):
-                send_s(j)
-            note("rs", ("lsi", total["lsi"]), [c("S")], [])
-            op("g", lambda: g.iota(ap(c("Q")), [[1, V]], 0, 0, allow_small_or_imprecise_dtypes=True), [], [c("Q")])
-            wait("s", ("lsi", total["lsi"]))
-            dma([("s", ap(c("NBI", 0, LR)), T.nb[:, 0:LR])], "ln0", [], [c("NBI", 0, LR)])
-            dma([("s", ap(c("TR")), T.tr[:])], "ltr", [], [c("TR")])
-            dma([("s", ap(c("NBI", LR, V)), T.nb[:, LR:V])], "ln1", [], [c("NBI", LR, V)])
-            for f in fl:
-                f()
-            fl = [ftab("S", "F", r, "B%d" % (i + 4), 0) for i, r in enumerate(halves("S", 2))]
-            w()
-            gather2(c("G1"), "XI", lst(0))
-            w = wrap("G1", LR, "W2", 0, "B7", lst(1))
-            for f in fl:
-                f()
-            fl = [ftab("S", "F", r, "B%d" % i, 0) for i, r in enumerate(halves("S", 3))]
-            w()
-            gather2(c("G0"), "XI", lst(1))
-            w = wrap("G0", LR, "W1", 0, "B6", lst(2))
-            for f in fl:
-                f()
-            f = htab(1, "B4")
-            gather("v", gv(FC3), "F", lst(1))
-            w()
-            f()
-            gather2(c("XN"), "XI", c("EXN"))
-            gather2(c("G0"), "XN", lst(2))
-        else:
-            gather2(c("G0"), "XP", c1(t))
-            w = wrap("G0", LR, "W0", 0, "B6", lst(0))
-            conv(t, "NBF")
-            w()
-            gather2(c("G1"), "XP", lst(0))
-            wd = wrap("G1", LR, "W1", t, "B7", lst(2))
-            wc = wrap("G1", LR, "W0", 0, "B6", lst(1))
-            gather2(gv(FC2), "F", lst(0))
-            gather2(c("XN", *L(t - 1)), "XI", c("NXN", 32 * (t - 1), 32 * t))
-            wd()
-            gather2(c("G0"), "XN", lst(2))
-            wc()
-        w = wrap("G0", LR, "W0", 0, "B7", lst(3))
-        if t == 0:
-            f = htab(2, "B2")
-            gather("v", gv(SC1), "S", c1(0))
-        else:
-            gather("v", gv(FD0), "FN", lst(2))
-            gather("a", c("FX", *L(t - 1)), "FN", c("NXN", 32 * (t - 1), 32 * t))
-        w()
-        gather2(c("G1"), "XN", lst(3))
-        w = wrap("G1", LR, "W0", 0, "B6", lst(4))
-        if t == 0:
-            f()
-            f = htab(3, "B3")
-        else:
-            gather("v", gv(FC3), "F", lst(1))
-            gather("a", gv(FD1), "FN", lst(3))
-        w()
-        if t == 0:
-            gather2(c("G0"), "XN", lst(4))
-            w = wrap("G0", LR, "W0", 0, "B7", lst(5))
-            f()
-            gather("a", gv(FC1), "F", c1(0))
-            gather("v", gv(FC2), "F", lst(0))
-            w()
-            pend = None
+            wrap("G1", 0, LR, W0, 0, "B6", lst(C3))
+            gather(c("G0"), "XP", lst(C3), parts=2)
+            wrap("G0", 0, LR, W1, 0, "B7", lst(D0))
+            spread("XN", "EHN")
+            own(0, "av")
             for j in range(NCH):
                 for h in range(2):
-                    f = ftab("SN", "FN", halves("SN", j)[h], "B%d" % ((2 * j + h) % 3), V, h == 1 and j % 2 == 0)
-                    if pend:
-                        pend()
-                    pend = f
-                if j in (1, 2):
-                    conv(0, ("NBU", "NBF")[j - 1])
-            pend()
-        wmm(t, 0)
-        wmm(t, 1)
-
-        tab1, l1 = ("FN", 5) if t == 0 else ("FX", 4)
-        for e, (lo, hi) in zip("aav", CH):
-            gather(e, gv(GX, lo, hi), tab1, lst(l1, lo, hi))
-        extra = {2: (SD0, "SN", 2), 3: (SC3, "S", 1), 4: (SC2, "S", 0)}
+                    ftab("SN", "NFN", halves("SN", j)[h], "B%d" % ((2 * j + h) % 4), V, 2 * j + h < OPT["npe"])
+        else:
+            wrap("G1", 0, LR, W1, t, "B6", lst(D0))
+            wrap("G1", 0, LR, W0, 0, "B7", lst(C3))
+            gather(c("XN", *L(t - 1)), "XI", c("NXN", 32 * (t - 1), 32 * t), parts=2)
+            for lo in (0, 256):
+                gtt(c("TD", lo, lo + 256), "NFN", c("NXN", 32 * (t - 1) + lo // 16, 32 * (t - 1) + lo // 16 + 16), c("GX", lo, lo + 256), SUB)
+                tt(c("FX", *L(t - 1, lo, lo + 256)), c("SN", *L(t - 1, lo, lo + 256)), c("TD", lo, lo + 256), SUB)
+        pre(5, 0, lst(C2))
+        pre(4, 0, lst(C3))
+        gather(c("G0"), "XN", lst(D0), parts=2)
+        wrap("G0", 0, LR, W0, 0, "B6", lst(D1))
+        pre(3, 1, lst(D0))
+        gather(c("G1"), "XN", lst(D1), parts=2)
+        wrap("G1", 0, LR, W0, 0, "B7", lst(D2))
+        pre(2, 1, lst(D1))
         if t == 0:
-            gather("v", gv(FD1), "FN", lst(3))
-            gather("a", gv(FD0), "FN", lst(2))
-        fs = {2: FD1, 3: FD0, 4: FC3, 5: FC2, 6: FC1}
-        ss = {3: SD0, 4: SC3, 5: SC2, 6: SC1}
-        fused = {1: 4, 2: 3}
-        order = []
-        for s in range(1, 9):
-            for i in range(3):
-                for j in range(3):
-                    if not (s == 1 and j == 0) and not (s == 8 and j == 2):
-                        order.append((9 * s + 3 * i + 2 * j, s, i, j))
-        for _, s, i, j in sorted(order):
-            lo, hi = CH[i]
-            b = c("B%d" % i, 0, hi - lo)
-            y = c("S", *L(t, lo, hi)) if s == 7 else c("Y", lo, hi)
-            if s == 8:
-                if j == 0:
-                    if t < R - 1:
-                        ts(c("B4", lo, hi), c("S", *L(t, lo, hi)), -1.0, 1.5, MUL, ADD)
-                else:
-                    tt(c("H", *L(t, lo, hi)), c("TA", lo, hi), b, ADD)
-                continue
-            if j == 0:
-                tt(b, b, c("TB", lo, hi), MUL)
-            elif j == 1:
-                if s == 1:
-                    gsub(c("TD", lo, hi), "FN", lst(4, lo, hi), gv(GX, lo, hi))
-                elif s in fused:
-                    tt(c("TD", lo, hi), gv(fs[s], lo, hi), b, SUB)
-                else:
-                    tt(b, b, gv(fs[s], lo, hi) if s < 7 else c("F", *L(t, lo, hi)), SUB)
-            else:
-                if s in fused:
-                    gsub(y, "SN", lst(fused[s], lo, hi), c("TD", lo, hi))
-                else:
-                    tt(y, b, gv(ss[s], lo, hi) if s < 7 else y, ADD)
-                if s == 3 and t > 0:
-                    rb = c("B%d" % (3 + i), 0, hi - lo)
-                    mm([(ap(rb), T.RB[:, 16 * t:16 * t + 128], ap(y), True, True)], [c("RB"), y], [rb])
-                    y = rb
-                if s < 7:
-                    av(b, y, SQ)
-                    av(c("TB", lo, hi), y, IDF, bias=1.5, scale=-1.0)
-                    if s + 1 in extra:
-                        o, tab, li = extra[s + 1]
-                        gather("a", gv(o, lo, hi), tab, lst(li, lo, hi))
-                else:
-                    av(c("TB", lo, hi), y, SQ, bias=1.0, scale=-1.0)
-                    av(c("TA", lo, hi), y, SQ)
-                    av(b, c("TB", lo, hi), IDF, scale=0.5)
-                if s == 3 and i == 2:
-                    if t < R - 1:
-                        need("g", "rc", [], [c("SN"), c("FN")])
-                        g.remote_sem_update(T.sem["cr%d" % t], T.sem.lsr, spid, srid, one)
-                        bump("lsr", 1)
-                    items = [(ap(c("B3")), ap(c("IDB", 0, 128)), ap(c("KC")), True, False)]
-                    for k in range(K):
-                        items.append((T.B3[:, k:LR:16], T.RB[:, 0:128], ap(c("NBF", t * LR + 32 * k, t * LR + 32 * k + 32)), False, False))
-                    mm(items, [c("IDB"), c("KC"), c("RB"), c("NBF", *L(t))], [c("B3")])
-        dma([("s", T.ys[:, t * LR:(t + 1) * LR], ap(c("S", *L(t))))], "outs", [c("S", *L(t))], [])
+            gather(c("G0"), "XN", lst(D2), parts=2)
+            wrap("G0", 0, LR, W0, 0, "B6", lst(D3))
+            wrap("XP", LR, V - LR, W0, 0, "B7", c("EXW", 32, 128))
+            wrap("XN", 0, V, W0, 0, "B6", c("EXN"))
+            for u in range(1, R):
+                sq(c("U", *L(u)), c("S", *L(u)), 1.0, -1.0)
+                lin(c("H", *L(u)), c("U", *L(u)), 0.5, 0.0)
+                dma("g", ap(c("H", *L(u))), ap(c("M", *L(u))), [c("M", *L(u)), c("H", *L(u))], [c("H", *L(u))], 3.5, after=[left], accum_op=ADD)
+        cp(c("NBU", *L(t)), c("NBI", *L(t)))
+        cp(c("NBF", *L(t)), c("NBI", *L(t)))
+        items = [(ap(c("B3")), ap(c("IDB", 0, 128)), ap(c("KC")), True, False)]
+        for k in range(K):
+            items.append((T.B3[:, k:LR:16], T.RB[:, 0:128], ap(c("NBF", t * LR + 32 * k, t * LR + 32 * k + 32)), False, False))
+        mm(items, LR + 16 * 256, [c("IDB"), c("KC"), c("RB"), c("NBF", *L(t))], [c("B3")])
 
-        def ug(k):
-            gather("a", c("U", (k % URING) * LR, (k % URING + 1) * LR), "H", c("NBU", t * LR + 32 * k, t * LR + 32 * k + 32))
+        early = []
+        for s in range(1, 9):
+            for i, (lo, hi) in enumerate(CH):
+                k = hi - lo
+                b, slot, mid = c(SB[i], LR - k, LR), c(SB[i], 0, 3 * k), T[SB[i]][:, 1:3 * k - 1:3]
+                if s == 1:
+                    mm([(ap(slot), T.IDB[:, 0:128], T.CP[:, 0:3 * k], True, True)], 3 * k, [c("IDB"), c("CP")], [slot])
+                if s == 1 and t > 0:
+                    y = c("Y", lo, hi)
+                    gather(y, "FX", lst(D2, lo, hi))
+                elif s == 1:
+                    gather(c("GX", lo, hi), "NFN", lst(D3, lo, hi))
+                    gtt(c("TD", lo, hi), "NFN", lst(D2, lo, hi), c("GX", lo, hi), SUB)
+                    y = c("Y", lo, hi)
+                    gtt(y, "SN", lst(D2, lo, hi), c("TD", lo, hi), ADD)
+                elif s < 8:
+                    o = 3 * LR * (s - 2)
+                    y = part("O", 2, 0, lo, hi)
+                    vop(lambda o=o, lo=lo, hi=hi, slot=slot: vec.tensor_tensor_scan(
+                        T.O[:, 3 * lo:3 * hi], ap(slot), T.D1[:, o + 3 * lo:o + 3 * hi], 0.0, MUL, ADD), 3 * k,
+                        [slot] + [part("D1", j, s - 2, lo, hi) for j in range(3)], [y])
+                else:
+                    continue
+                if s == 7:
+                    new = c("S", *L(t, lo, hi))
+                    gop(lambda new=new, y=y, k=k: g.affine_select(ap(new), ap(y), [[0, k]], GE, 0.0, 0, 0), k, [y], [new])
+                    if t < R - 1:
+                        mm([(mid, T.IDB[:, 384:512], T.CP[:, 1:3 * k - 1:3], True, False), (mid, T.RB[:, 0:128], ap(y), False, True)],
+                           5 * k, [c("IDB"), c("CP"), c("RB"), y], [slot])
+                    sq(c("TB", lo, hi), y, 1.0, -1.0)
+                    sq(c("TA", lo, hi), y)
+                    lin(b, c("TB", lo, hi), 0.5, 0.0, OPT["q2"])
+                    tt(c("H", *L(t, lo, hi)), c("TA", lo, hi), b, ADD)
+                    if t < R - 1:
+                        early.append(vop(lambda mid=mid, lo=lo, hi=hi, t=t: vec.tensor_tensor(ap(c("NF", *L(t, lo, hi))), T.TA[:, lo:hi], mid, MUL), k,
+                                         [slot, c("TA", lo, hi)], [c("NF", *L(t, lo, hi))]))
+                    continue
+                if s == 3 and t > 0:
+                    mm([(ap(b), T.RB[:, 16 * t:16 * t + 128], ap(y), True, True)], 4 * k, [c("RB"), y], [b])
+                    y = b
+                sq(part("D1", 0, s - 1, lo, hi), y)
+                if (s, i) in OPT["peb"] and not psum(y):
+                    mm([(mid, T.IDB[:, 0:128], T.CP[:, 1:3 * k - 1:3], True, False), (mid, T.RBN[:, :], ap(y), False, True)],
+                       5 * k, [c("IDB"), c("CP"), c("RBN"), y], [slot])
+                else:
+                    add([("a", ca(k), lambda mid=mid, y=y: act.activation(mid, ap(y), IDF, bias=1.5, scale=-1.0))], [y], [slot])
+        dma("s", T.ys[:, t * LR:(t + 1) * LR], ap(c("S", *L(t))), [c("S", *L(t))], [], 3.0)
+        if t < R - 1:
+            cr = add([("g", 0.3, lambda t=t: g.remote_sem_update(T.sem["cr%d" % t], T.sem.lsr, spid, srid, one))], [], [c("SN"), c("NFN")],
+                     0.0, None, (), False)
+            bump("lsr", 1)
+            ok = event("cr%d" % t, 1, 2.0, [cr])
+            s_ = remote(lambda t=t: g.remote_dma_fused([
+                RemoteDMATransfer(dst_ids=[DstId(rid=prid, pnc=ppid)], dma_engine_mask=m, remote_sem=T.sem["sf%d" % t],
+                                  src=ap(c(a, *L(t))), dst=ap(c(a + "N", *L(t)))) for a, m in (("S", pm_a), ("NF", pm_b))], local_sem=T.sem.lsr),
+                [c("S", *L(t)), c("NF", *L(t))], [ok])
+            bump("lsr", bits(pm))
+            event("sf%d" % t, n_s, 12.0, [s_], writes=[c("SN", *L(t)), c("NFN", *L(t))])
+            dma("s", ap(c("GX")), ap(c("NFN", *L(t))), [c("NFN", *L(t))], [c("GX")])
 
         def mk(k):
             return c("M", k * LR, (k + 1) * LR)
-        gather2(c("U", 0, LR), "H", c("NBU", t * LR, t * LR + 32))
-        if t < R - 1:
-            tt(c("F", *L(t)), c("TA"), c("B4"), MUL)
-            g.wait_ge(T.sem["cr%d" % t], 1)
-            waited["g"]["cr%d" % t] = 1
-            bump("cr%d" % t, 1)
-            need("g", "rf", [c("S", *L(t)), c("F", *L(t))], [])
-            g.remote_dma_fused([
-                RemoteDMATransfer(dst_ids=[DstId(rid=prid, pnc=ppid)], dma_engine_mask=pm_a, remote_sem=T.sem["sf%d" % t],
-                                  src=ap(c("S", *L(t))), dst=ap(c("SN", *L(t)))),
-                RemoteDMATransfer(dst_ids=[DstId(rid=prid, pnc=ppid)], dma_engine_mask=pm_b, remote_sem=T.sem["sf%d" % t],
-                                  src=ap(c("F", *L(t))), dst=ap(c("FN", *L(t))))], local_sem=T.sem.lsr)
-            bump("lsr", bits(pm))
-            arrival("sf%d" % t, n_s, [c("SN", *L(t)), c("FN", *L(t))])
-        wmm(t, 2)
-        wmm(t, 3)
-        for k in range(1, URING):
-            ug(k)
         for k in range(K + 1):
             if k < K:
-                b = c(WR[k % 4])
-                tt(mk(0) if k == 0 else b, c("U", (k % URING) * LR, (k % URING + 1) * LR), b, MUL)
-                if k + URING < K:
-                    ug(k + URING)
-                if k == 0:
-                    wmm(t, 4)
+                b, u = c(WR[k % 4]), c("U", (k % URING) * LR, (k % URING + 1) * LR)
+                mm([(ap(b), ap(c("BS", 128 * k, 128 * k + 128)), ap(c("TR", *L(t))), True, True)], LR, [c("BS"), c("TR")], [b])
+                ls = c("NBU", t * LR + 32 * k, t * LR + 32 * k + 32)
+                if k < OPT["u0"]:
+                    gather((u[0], u[1], u[1] + 256), "H", (ls[0], ls[1], ls[1] + 16), "v")
+                    gather((u[0], u[1] + 256, u[2]), "H", (ls[0], ls[1] + 16, ls[2]), "a")
+                else:
+                    hint.extend([last_u] if k else [])
+                    gather(u, "H", ls, "a")
+                last_u = len(ops) - 1
+                if k == OPT["nf"]:
+                    hint.extend(early)
+                tt(mk(0) if k == 0 else b, u, b, MUL)
             if k >= 2:
                 b = c(WR[(k - 1) % 4])
                 tt(mk(k - 1) if k - 1 < 15 else b, mk(k - 2), b, MAX)
-                if k + 3 < K:
-                    wmm(t, k + 3)
         mf = c(WR[15 % 4])
-        idle = []
         if t < R - 1:
-            gather("a", gv(FC1), "F", c1(t + 1))
-            gather("a", gv(SC1), "S", c1(t + 1))
-            if t == 0:
-                idle += [(c("XP", *L(u)), "XI", c1(u)) for u in range(1, R)]
+            own(t + 1, "a")
             for u in range(R):
                 if u != t:
-                    idle.append((c("FX", *L(u)), "FN", c("NXN" if u < t else "EXN", 32 * u, 32 * u + 32)))
+                    ls, fx = c("NXN" if u < t else "EXN", 32 * u, 32 * u + 32), c("FX", *L(u))
+                    add([("a", 0.065 + LR * GAT * CYC, lambda ls=ls, fx=fx: act.activation(ap(fx), ind("NFN", ls), CPY, scale=-1.0))], [c("NFN"), ls], [fx])
+                    for a in ("NFN", "SN"):
+                        dma("g", ap(fx), ap(c(a, *L(u))), [c(a, *L(u)), fx], [fx], 3.5, accum_op=ADD)
+                    if t == 0:
+                        gather(c("XP", *L(u)), "XI", c1(u), "a")
         else:
             for u in range(t):
-                gather("a", c("XO", *L(u)), "Q", c("NXO", 32 * u, 32 * u + 32))
-            dma([("s", T.yx[:, 0:t * LR], T.XO[0:128:16, 0:t * LR])], "outs", [c("XO", 0, t * LR)], [])
+                hint.append(last_u)
+                gather(c("XO", *L(u)), "Q", c("NXO", 32 * u, 32 * u + 32), "a")
+            dma("s", T.yx[:, 0:t * LR], T.XO[0:128:16, 0:t * LR], [c("XO", 0, t * LR)], [], 2.0)
         groups = [(k, min(k + 2, 15)) for k in range(0, 15, 2)]
-
-        def vupd(k0, k1):
+        for j, (k0, k1) in enumerate(groups):
+            for k in range(k0, k1):
+                tt(c("Z", k * LR, (k + 1) * LR), mk(k), mf, GE)
+            cb = c(CR[j % 3], 0, 32 * (k1 - k0))
+            mm([(ap(cb), T.WS[:, VB + 15 - a:VB + 143 - a], T.Z[:, k0 * LR + a:k1 * LR:16], a == 0, a == 15) for a in range(16)],
+               16 * 64, [c("WS"), c("Z", k0 * LR, k1 * LR)], [cb])
+            lin(c("CS", 32 * k0, 32 * k1), cb, 1.0, 0.0, "a")
             items = []
             for k in range(k0, k1):
                 items.append((T.B3[:, k:LR:16], ap(c("IDB", 128, 256)), ap(c("CS", 32 * k, 32 * k + 32)), False, False))
                 items.append((T.B3[:, k + 1:LR:16], ap(c("IDB", 256, 384)), ap(c("CS", 32 * k, 32 * k + 32)), False, k == 14))
-            mm(items, [c("IDB"), c("CS", 32 * k0, 32 * k1)], [c("B3")])
-        for j, (k0, k1) in enumerate(groups):
-            for k in range(k0, k1):
-                tt(c("Z", k * LR, (k + 1) * LR), mk(k), mf, GE)
-            cb = c(CR[j % 6], 32 * k0, 32 * k1)
-            mm([(ap(cb), T.VB[:, 15 - a:143 - a], T.Z[:, k0 * LR + a:k1 * LR:16], a == 0, a == 15) for a in range(16)],
-               [c("VB"), c("Z", k0 * LR, k1 * LR)], [cb])
-            if j > 0:
-                vupd(*groups[j - 1])
-            if idle:
-                gather("a", *idle.pop(0))
-            av(c("CS", 32 * k0, 32 * k1), cb, CPY)
-        vupd(*groups[-1])
-        if t < R - 1:
-            conv(t + 1, "NBU")
-        op("v", lambda: vec.tensor_tensor_scan(ap(c("BM")), ap(c("RM")), ap(c("B3")), 0.0, MUL, MAX), [c("RM"), c("B3")], [c("BM")])
-        op("v", lambda: vec.tensor_copy(ap(c("XA")), T.BM[:, 15:LR:16]), [c("BM")], [c("XA")])
-        ts(c("XB"), c("XA"), 2047, None, AND)
+            mm(items, 64 * len(items), [c("IDB"), c("CS", 32 * k0, 32 * k1)], [c("B3")])
+        vop(lambda: vec.tensor_tensor_scan(ap(c("BM")), ap(c("RM")), ap(c("B3")), 0.0, MUL, MAX), LR, [c("RM"), c("B3")], [c("BM")])
+        vop(lambda: vec.tensor_copy(ap(c("XA")), T.BM[:, 15:LR:16]), 32, [c("BM")], [c("XA")])
+        ts(c("XB"), c("XA"), 2047, AND)
         nx = c("NXO", 32 * t, 32 * t + 32)
         cp(nx, c("XB"))
         if t < R - 1:
-            need("g", "rn", [nx], [])
-            g.remote_dma(ap(c("NXN", nx[1], nx[2])), ap(nx), T.sem["nx%d" % t], T.sem.lsr, ppid, prid, pm)
+            s_ = remote(lambda t=t, nx=nx: g.remote_dma(ap(c("NXN", nx[1], nx[2])), ap(nx), T.sem["nx%d" % t], T.sem.lsr, ppid, prid, pm), [nx])
             bump("lsr", bits(pm))
-            arrival("nx%d" % t, n_s, [c("NXN", nx[1], nx[2])])
-            gather2(c("XP", *L(t)), "XI", nx)
+            event("nx%d" % t, n_s, OPT["nx"], [s_], writes=[c("NXN", nx[1], nx[2])])
+            gather(c("XP", *L(t)), "XI", nx, parts=2)
         else:
-            gather2(c("XO", *L(t)), "Q", nx)
-            dma([("s", T.yx[:, t * LR:V], T.XO[0:128:16, t * LR:V])], "outs", [c("XO", *L(t))], [])
+            gather(c("XO", *L(t)), "Q", nx, parts=2)
+            dma("s", T.yx[:, t * LR:V], T.XO[0:128:16, t * LR:V], [c("XO", *L(t))], [], 2.0)
 
+    known = {e: {} for e in Qs}
+    for o in lay_out(ops):
+        e = o["eng"]
+        if e == "x":
+            o["clock"] = dict([o["tok"]])
+            continue
+        for d in sorted(o["deps"], key=lambda d: -ops[d]["start"]):
+            p = ops[d]
+            if p["tok"] is None or e == p["eng"] == "p" or known[e].get(p["tok"][0], 0) >= p["tok"][1]:
+                continue
+            Qs[e].wait_ge(T.sem[p["tok"][0]], p["tok"][1])
+            for s, v in p["clock"].items():
+                known[e][s] = max(known[e].get(s, 0), v)
+        ins = o["fn"]()
+        if o["tok"] == "own":
+            o["tok"] = bump("c" + e, 1)
+            ins.then_inc(T.sem["c" + e], 1)
+        if o["tok"] is not None:
+            o["clock"] = dict(known[e], **dict([o["tok"]]))
     for s in sorted(total):
-        wait("g", (s, total[s]))
+        g.wait_ge(T.sem[s], total[s])

@@ -2,8 +2,10 @@ from concourse.bass import DstId, RemoteDMATransfer
 from concourse.mybir import AluOpType, ActivationFunctionType
 
 V, K, R, LR = 2048, 16, 4, 512
-NCH = 2
-CW = V // (2 * NCH)
+NEAR, FAR, DIRECT = 0, 1, 2
+SENDS = [[(0, 256, FAR, 11.0)], [(256, 768, FAR, 11.0)], [], [(768, 1024, FAR, 11.0), (1024, 1280, DIRECT, 7.0)],
+         [(1280, 1792, DIRECT, 8.0)], [(1792, 2048, DIRECT, 8.5)]]
+LOADS = [(0, 256), (256, 256), (256, 768), (768, 1280), (1280, 1792), (1792, 2048)]
 URING = 6
 CH = [(0, 128), (128, 256), (256, 384), (384, 512)]
 F32, BF, I32, U16 = "float32", "bfloat16", "int32", "uint16"
@@ -13,9 +15,10 @@ for _n in ("S", "NF", "H", "SN", "NFN", "FX", "Q", "XO", "NBF"):
     SCRATCH[_n] = ("sbuf", [128, V], F32)
 for _n in ("XI", "XP", "XN", "CL", "TR", "BS"):
     SCRATCH[_n] = ("sbuf", [128, V], BF)
-for _n in ("Y", "GX", "TA", "TB", "TD", "BM"):
+for _n in ("Y", "TA", "TB", "TD"):
     SCRATCH[_n] = ("sbuf", [128, LR], F32)
-for _n in ("G0", "G1", "EH", "EHN", "SP", "KC", "RM", "CS", "IDB"):
+SCRATCH["BM"] = ("sbuf", [128, LR], I32)
+for _n in ("G0", "G1", "EH", "EHN", "SP", "KC", "RM", "CS", "IDB", "W0S"):
     SCRATCH[_n] = ("sbuf", [128, LR], BF)
 for _n in ("EXW", "EXN", "NXO", "NXN"):
     SCRATCH[_n] = ("sbuf", [128, 128], U16)
@@ -25,22 +28,23 @@ SCRATCH.update({
     "D1": ("sbuf", [128, 6 * 3 * LR], F32), "O": ("sbuf", [128, 3 * LR], F32),
     "LS": ("sbuf", [128, 6 * 32], U16), "EC": ("sbuf", [128, LR], I32), "WS": ("sbuf", [128, 768], BF),
     "I0": ("sbuf", [128, 176], I32), "I1": ("sbuf", [128, 80], I32), "RB": ("sbuf", [128, 176], F32),
-    "RBN": ("sbuf", [128, 128], F32), "CP": ("sbuf", [128, 384], BF), "C15": ("sbuf", [128, 256], BF), "XA": ("sbuf", [128, 32], I32), "XB": ("sbuf", [128, 32], I32),
+    "RBN": ("sbuf", [128, 128], F32), "CP": ("sbuf", [128, 384], BF), "C15": ("sbuf", [128, 256], BF), "CQ": ("sbuf", [128, 384], BF),
+    "XB": ("sbuf", [128, 32], I32),
 })
 for _b in range(8):
     SCRATCH["B%d" % _b] = ("psum", [128, 512], F32)
 
 NDMA = 48
 SEMAPHORES = (["cv", "ca", "cp", "cg", "lsi", "lsr", "aeh"] + ["d%d" % j for j in range(NDMA)]
-              + [s + str(j) for s in ("ad", "ah", "hh") for j in range(4)]
-              + [s + str(t) for s in ("sf", "nx", "cr") for t in range(R - 1)])
+              + [s + str(j) for s in ("ad", "hh") for j in range(8)]
+              + [s + str(t) for s in ("sf", "nx", "cr", "xp", "yp", "yl") for t in range(R - 1)])
 
 ADD, SUB, MUL, MAX = AluOpType.add, AluOpType.subtract, AluOpType.mult, AluOpType.max
 AND, SHR, EQ, GE = AluOpType.bitwise_and, AluOpType.arith_shift_right, AluOpType.is_equal, AluOpType.is_ge
 SQ, IDF, CPY = ActivationFunctionType.Square, ActivationFunctionType.Identity, ActivationFunctionType.Copy
 
-CYC, PEC, GAT, HOP = 0.83e-3, 0.62e-3, 1.56, 0.1
-OPT = dict(first=10.0, step=1.5, pp=2, fb=40, q2="a", on={}, nx=2.6, peb=[(s, i) for s in (1, 2) for i in range(4)], u0=1, nf=2, seed=1, amp=1.5, win=5.0, fpe=0, npe=0)
+CYC, PEC, GAT, HOP = 0.83e-3, 0.6e-3, 1.65, 0.19
+OPT = dict(hl=[(0, 512)], first=-1.0, step=1.5, pp=2, fb=40, q2="av", on={}, nx=2.6, peb=[(s, i) for s in range(1, 7) for i in range(4) if (s + i) % 2 == 0], peb0=[(s, i) for s in range(1, 7) for i in range(4) if (s + i) % 2 == 0], xnd=1, bv=(), cv=1, pt=1, sf=9.5, xs=1, ys=320, yl=0.8, eh=4.5, pend=0, w0=6, u0=0, nf=2, seed=1, amp=0.6, win=3.0, fpe=0, npe=0)
 PLAN = []
 
 
@@ -51,18 +55,21 @@ def bits(m):
 def helpers_of(c, dst, T, topo):
     free = [h for h in topo.cores_of(c) if T.rank_of(h) is None and topo.may_write(h, dst) and topo.addr(h)[2] != topo.addr(c)[2]]
     hs = [[h for h in free if topo.die(h) == topo.die(c)][0], [h for h in free if topo.die(h) != topo.die(c)][0]]
-    es = topo.engines(c, hs[0])
-    return hs, [sum(1 << e for e in es[0::2]), sum(1 << e for e in es[1::2])]
+    ways = {p[2] for call in SENDS for p in call}
+    es = [e for e in topo.engines(c, hs[0]) if DIRECT not in ways or e not in topo.engines(c, dst)]
+    a, b = (es[0::2], es[1::2]) if {NEAR, FAR} <= ways else (es, es)
+    return hs, [sum(1 << e for e in a), sum(1 << e for e in b), topo.mask(c, dst)]
 
 
-def helper_program(g, core, half, n_in, dst, T, topo):
+def helper_program(g, core, way, n_in, dst, T, topo):
     rid, pid, _ = topo.addr(dst)
     m = topo.mask(core, dst)
-    for j in range(NCH):
-        lo = half * (V // 2) + j * CW
+    mine = [(j, p) for j, p in enumerate(p for call in SENDS for p in call) if p[2] == way]
+    for j, (lo, hi, _, _) in mine:
         g.wait_ge(T.sem["hh%d" % j], n_in)
-        g.remote_dma(T.SN[:, lo:lo + CW], T.S[:, lo:lo + CW], T.sem[("ad%d", "ah%d")[half] % j], T.sem.lsi, pid, rid, m)
-    g.wait_ge(T.sem.lsi, NCH * bits(m))
+        g.remote_dma(T.SN[:, lo:hi], T.S[:, lo:hi], T.sem["ad%d" % j], T.sem.lsi, pid, rid, m)
+    if mine:
+        g.wait_ge(T.sem.lsi, len(mine) * bits(m))
 
 
 def lay_out(ops):
@@ -155,7 +162,7 @@ def rank_program(g, core, T, topo):
         return
     pred, succ = T.cores[(rank - 1) % n], T.cores[(rank + 1) % n]
     hs, hm = helpers_of(core, pred, T, topo)
-    hid = [DstId(rid=topo.addr(h)[0], pnc=topo.addr(h)[1]) for h in hs]
+    hid = [DstId(rid=topo.addr(h)[0], pnc=topo.addr(h)[1]) for h in hs + [pred]]
     prid, ppid, _ = topo.addr(pred)
     srid, spid, _ = topo.addr(succ)
     pm = topo.mask(core, pred)
@@ -163,7 +170,7 @@ def rank_program(g, core, T, topo):
     pm_a = sum(1 << e for e in pe[:len(pe) // 2])
     pm_b = pm & ~pm_a
     n_s = bits(topo.mask(succ, core))
-    n_h = [bits(topo.mask(h, core)) for h in helpers_of(succ, core, T, topo)[0]]
+    n_h = [bits(topo.mask(h, core)) for h in helpers_of(succ, core, T, topo)[0] + [succ]]
     one = 1 << topo.engines(core, succ)[0]
     vec, act, pe_ = g.vector, g.scalar, g.tensor
     Qs = {"v": vec, "a": act, "p": pe_, "g": g, "s": g.sync}
@@ -233,10 +240,10 @@ def rank_program(g, core, T, topo):
         return r[2] - r[1]
 
     def cv(k):
-        return 0.03 + max(64, k) * CYC
+        return 0.01 + max(64, k) * CYC
 
     def ca(k):
-        return 0.05 + max(64, k) * CYC
+        return 0.015 + max(64, k) * CYC
 
     def vop(fn, k, reads, writes, **kw):
         return add([("v", cv(k), fn)], reads, writes, **kw)
@@ -244,8 +251,11 @@ def rank_program(g, core, T, topo):
     def gop(fn, k, reads, writes, **kw):
         return add([("g", 0.14 + 2 * k * CYC, fn)], reads, writes, **kw)
 
-    def tt(o, a, b, f):
-        return vop(lambda: vec.tensor_tensor(ap(o), ap(a), ap(b), f), w(o) * (1 if psum(a) or psum(b) else 2), [a, b], [o])
+    def tt(o, a, b, f, parts=1):
+        for p in range(parts):
+            h = w(o) // parts
+            oo, aa, bb = [(r[0], r[1] + p * h, r[1] + (p + 1) * h) for r in (o, a, b)]
+            vop(lambda oo=oo, aa=aa, bb=bb: vec.tensor_tensor(ap(oo), ap(aa), ap(bb), f), h * (1 if psum(a) or psum(b) else 2), [aa, bb], [oo])
 
     def ts(o, a, s1, f0, oap=None):
         vop(lambda: vec.tensor_scalar(oap if oap is not None else ap(o), ap(a), s1, None, f0), w(a), [a], [o])
@@ -264,16 +274,17 @@ def rank_program(g, core, T, topo):
     def ind(tab, ls):
         return T[tab][:, 0:V].indirect(ap(ls))
 
-    def gather(o, tab, ls, on="av", parts=1):
+    def gather(o, tab, ls, on="av", parts=1, scale=1.0):
         for p in range(parts):
             h, k = w(o) // parts, w(ls) // parts
             oo, ll = (o[0], o[1] + p * h, o[1] + (p + 1) * h), (ls[0], ls[1] + p * k, ls[1] + (p + 1) * k)
-            opts = {"a": ("a", 0.065 + h * GAT * CYC, lambda oo=oo, ll=ll: act.activation(ap(oo), ind(tab, ll), CPY)),
-                    "v": ("v", 0.05 + h * GAT * CYC, lambda oo=oo, ll=ll: vec.tensor_copy(ap(oo), ind(tab, ll)))}
+            opts = {"a": ("a", 0.065 + h * GAT * CYC, lambda oo=oo, ll=ll: act.activation(ap(oo), ind(tab, ll), CPY, scale=scale)),
+                    "v": ("v", 0.05 + h * GAT * CYC, lambda oo=oo, ll=ll: vec.tensor_copy(ap(oo), ind(tab, ll)) if scale == 1.0 else
+                          vec.tensor_scalar(ap(oo), ind(tab, ll), scale, None, MUL))}
             add([opts[e] for e in on], [c(tab), ll], [oo])
 
     def gtt(o, tab, ls, b, f):
-        add([("v", 0.05 + w(o) * GAT * CYC, lambda: vec.tensor_tensor(ap(o), ind(tab, ls), ap(b), f))], [c(tab), ls, b], [o])
+        add([("v", 0.05 + w(o) * 2 * CYC, lambda: vec.tensor_tensor(ap(o), ind(tab, ls), ap(b), f))], [c(tab), ls, b], [o])
 
     def mm(items, cyc, reads, writes):
         def fn():
@@ -308,15 +319,13 @@ def rank_program(g, core, T, topo):
         kw = {} if o[0] in ("I0", "I1") else {"allow_small_or_imprecise_dtypes": True}
         return gop(lambda: g.iota(ap(o), pattern, base, cm, **kw), w(o), [], [o], after=after)
 
-    def halves(b, j):
-        return [c(b, h * (V // 2) + j * CW, h * (V // 2) + (j + 1) * CW) for h in range(2)]
-
-    for q in range(4):
-        dma("sa"[q % 2], T.EC[32 * q:32 * q + 32, :], (T.ex, T.pt)[q % 2][:], [], [("EC%d" % q, 0, 1)], 2.0)
-    for j in range(NCH):
-        for h, r in enumerate(halves("S", j)):
-            hint.extend(range(len(ops)))
-            dma("s", ap(r), T.sat[:, r[1]:r[2]], [], [r], 2.4 + 2.0 / NCH * (2 * j + h + 1))
+    for x, (lo, hi) in enumerate(LOADS):
+        hint.extend(range(len(ops)))
+        if lo == hi:
+            for q in range(4):
+                dma("sa"[q % 2], T.EC[32 * q:32 * q + 32, :], (T.ex, T.pt)[q % 2][:], [], [("EC%d" % q, 0, 1)], 2.0 + lo / 800)
+        else:
+            dma("s", T.S[:, lo:hi], T.sat[:, lo:hi], [], [c("S", lo, hi)], 1.9 + hi / 800)
     iota(c("I1", 0, 32), [[-1, 4], [-4, 8]], 0, 1)
     iota(c("I1", 32, 48), [[0, 2], [-16, 8]], 0, 1)
     iota(c("I0"), [[1, 176]], 0, -1)
@@ -339,19 +348,23 @@ def rank_program(g, core, T, topo):
             mm([(ap(b), T.SP[:, 128 * a:128 * a + 128], ap(c(src)), True, True)], LR, [c("SP"), c(src)], [b])
             lin(c(dst, *L(a)), b, 1.0, 0.0)
     spread("XP", "EH")
-    s_ = remote(lambda: g.remote_dma(ap(c("EHN")), ap(c("EH")), T.sem.aeh, T.sem.lsr, ppid, prid, pm), [c("EH")], cost=1.5)
-    bump("lsr", bits(pm))
-    event("aeh", n_s, 3.0, [s_], writes=[c("EHN")])
-    sends = []
-    for j in range(NCH):
-        ab = halves("S", j)
-        s_ = remote(lambda ab=ab, j=j: g.remote_dma_fused(
-            [RemoteDMATransfer(dst_ids=[hid[h]], dma_engine_mask=hm[h], remote_sem=T.sem["hh%d" % j], src=ap(ab[h]), dst=ap(ab[h]))
-             for h in range(2)], local_sem=T.sem.lsi), ab, after=[s_])
+    sends, pieces = [], []
+    for call in SENDS:
+        if not call:
+            sends.append(remote(lambda: g.remote_dma(ap(c("EHN")), ap(c("EH")), T.sem.aeh, T.sem.lsr, ppid, prid, pm), [c("EH")], sends[-1:], 0.3 if sends else 1.5))
+            bump("lsr", bits(pm))
+            event("aeh", n_s, OPT["eh"], sends[-1:], writes=[c("EHN")])
+            continue
+        mine = list(enumerate(call, len(pieces)))
+        pieces += call
+        s_ = remote(lambda mine=mine: g.remote_dma_fused(
+            [RemoteDMATransfer(dst_ids=[hid[h]], dma_engine_mask=hm[h], remote_sem=T.sem[("ad%d" if h == DIRECT else "hh%d") % j],
+                               src=T.S[:, lo:hi], dst=T["SN" if h == DIRECT else "S"][:, lo:hi]) for j, (lo, hi, h, _) in mine],
+            local_sem=T.sem.lsi), [c("S", p[0], p[1]) for p in call], sends[-1:], 0.5 if sends else 1.5)
         sends.append(s_)
-        for h in range(2):
-            event(("ad%d", "ah%d")[h] % j, n_h[h], OPT["first"] + j * OPT["step"], [s_], writes=[halves("SN", j)[h]])
-    left = event("lsi", NCH * (bits(hm[0]) + bits(hm[1])), 5.0, sends, reads=[c("S")])
+        for j, (lo, hi, h, lat) in mine:
+            event("ad%d" % j, n_h[h], lat + OPT["first"], [s_], writes=[c("SN", lo, hi)])
+    left = event("lsi", sum(bits(hm[p[2]]) for p in pieces), 5.0, sends, reads=[c("S")])
     wrap("XP", 0, LR, W0, 0, "B6", c1(0))
 
     ts(c("RB", 0, 128), c("I0", 0, 128), 0.0, EQ)
@@ -371,29 +384,22 @@ def rank_program(g, core, T, topo):
             lin(c(b, 0, hi - lo), c(src, lo, hi), 1.0, -1.5)
         tt(c(dst, lo, hi), c("M", keep + lo, keep + hi), c(b, 0, hi - lo), MUL)
 
-    for i, u in enumerate((0, 2, 1, 3)):
+    for i, u in enumerate((0, 1, 2, 3)):
         ftab("S", "NF", c("S", *L(u)), "B%d" % (4 + i % 2), 0, i < OPT["fpe"])
     lin(c("RBN"), c("RB", 0, 128), -1.0, 0.0)
     for j, s in enumerate((0.0, 1.5, 1.0)):
         vop(lambda j=j, s=s: vec.memset(T.CP[:, j:384:3], s), 64, [], [c("CP")])
-    iota(c("KC"), [[0, 32], [-2048, 16]], 30720, 0, after=sends)
+    vop(lambda: vec.memset(ap(c("CQ")), 1.0), 192, [], [c("CQ")])
+    vop(lambda: vec.memset(T.CQ[:, 0:384:3], 0.0), 64, [], [c("CQ")])
+    hint.append(iota(c("XN"), [[0, V]], 0, 0, after=sends))
+    iota(c("BS"), [[0, V]], 1, 0, after=sends)
+    bs = gop(lambda: g.affine_select(ap(c("BS")), ap(c("BS")), [[-1, 16], [-16, 8], [0, 16]], EQ, 0.0, 0, 1), V, [c("BS")], [c("BS")])
+    iota(c("KC"), [[0, 32], [-2048, 16]], 30720, 0, after=[bs])
     vop(lambda: vec.memset(T.KC[:, 15:LR:16], 524288.0), 32, [], [c("KC")])
     vop(lambda: vec.memset(ap(c("RM")), 1.0), 256, [], [c("RM")])
     vop(lambda: vec.memset(T.RM[:, 0:LR:16], 0.0), 32, [], [c("RM")])
-    iota(c("BS"), [[0, V]], 1, 0, after=sends)
-    gop(lambda: g.affine_select(ap(c("BS")), ap(c("BS")), [[-1, 16], [-16, 8], [0, 16]], EQ, 0.0, 0, 1), V, [c("BS")], [c("BS")])
-    iota(c("XI"), [[16, 128], [0, 16]], 0, 0, after=sends)
-    iota(c("CL"), [[0, 128], [1, 16]], 0, 0, after=sends)
-    iota(c("Q"), [[1, V]], 0, 0, after=sends)
-    dma("s", ap(c("NBI", 0, LR)), T.nb[:, 0:LR], [], [c("NBI", 0, LR)], after=[left])
-    dma("s", ap(c("TR")), T.tr[:], [], [c("TR")], 4.0, after=[left])
-    dma("s", ap(c("NBI", LR, V)), T.nb[:, LR:V], [], [c("NBI", LR, V)], 6.0, after=[left])
-    xi = [dma("s", T.XI[1:128:16, :], T.CL[0:8, :], [c("CL"), c("XI")], [("XI1", 0, 1)])]
-    for r in (2, 3):
-        xi.append(dma("s", T.XI[r:128:16, :], T.XP[r:128:16, :], [c("XP"), c("XI")], [("XI%d" % r, 0, 1)]))
-    for i in xi:
-        recs["XI"].append((0, V, "w", i))
 
+    YS = OPT["ys"]
     WR = ["B5", "B6", "B7", "B4"]
     SB = ["B0", "B1", "B2", "B4"]
     CR = ["B0", "B1", "B2"]
@@ -403,54 +409,71 @@ def rank_program(g, core, T, topo):
         gather(part("D1", 1, s - 2), ("NF", "NFN")[far], ls, a, OPT["pp"])
         gather(part("D1", 2, s - 2), ("S", "SN")[far], ls, b, OPT["pp"])
 
-    def own(t, on):
+    def own(t, on, behind=()):
         pre(6, 0, c1(t), on)
         for j, a in ((1, c("NF", *L(t))), (2, c("S", *L(t)))):
+            hint.extend(behind)
             gop(lambda j=j, a=a: g.affine_select(ap(part("D1", j, 5)), ap(a), [[0, LR]], GE, 0.0, 0, 0), LR, [a], [part("D1", j, 5)])
 
     for t in range(R):
-        gather(c("G0"), "XP", c1(t), parts=2)
-        wrap("G0", 0, LR, W0, 0, "B7", lst(C2))
-        gather(c("G1"), "XP", lst(C2), parts=2)
+        HL = OPT["hl"] if t else [(0, LR)]
+        begun = [r[3] for r in recs.get("NXO", []) if r[2] == "w"] if OPT["cv"] else []
+
+        def follow(buf, tab, src, outs):
+            for h, (lo, hi) in enumerate(HL):
+                gather(c(buf, lo, hi), tab, (src[0], src[1] + lo // 16, src[1] + hi // 16), parts=2)
+                for x, (sel, rot, dst) in enumerate(outs):
+                    wrap(buf, lo, hi - lo, sel, rot, (("B6", "B7") if x == 0 or t == 0 else ("B0", "B1"))[h], lst(dst, lo, hi))
+        follow("G0", "XP", c1(t), [(W0, 0, C2)])
         if t == 0:
-            wrap("G1", 0, LR, W0, 0, "B6", lst(C3))
-            gather(c("G0"), "XP", lst(C3), parts=2)
-            wrap("G0", 0, LR, W1, 0, "B7", lst(D0))
-            spread("XN", "EHN")
+            follow("G1", "XP", lst(C2), [(W0, 0, C3)])
+            follow("G0", "XP", lst(C3), [(W1, 0, D0)])
+            if OPT["xnd"]:
+                xs = [dma("s", T.XN[r:128:16, :], T.EHN[64 * r:64 * r + 32, :], [c("EHN"), c("XN")], [("XN%d" % r, 0, 1)], 1.8) for r in range(2)]
+                recs["XN"] += [(0, V, "w", i) for i in xs]
+            else:
+                spread("XN", "EHN")
             own(0, "av")
-            for j in range(NCH):
-                for h in range(2):
-                    ftab("SN", "NFN", halves("SN", j)[h], "B%d" % ((2 * j + h) % 4), V, 2 * j + h < OPT["npe"])
+            copies = [len(ops) - 2, len(ops) - 1]
+            for b, lo, hi, lat in (("TR", 0, V, 4.0), ("NBI", 0, LR, 2.5), ("NBI", LR, V, 6.0)):
+                hint.extend(xs)
+                dma("s", ap(c(b, lo, hi)), (T.tr if b == "TR" else T.nb)[:, lo:hi], [], [c(b, lo, hi)], lat, after=[left])
+            for j, p in enumerate(sorted(pieces, key=lambda p: p[3] + 0.3 * pieces.index(p))):
+                for lo in range(p[0], p[1], 256):
+                    ftab("SN", "NFN", c("SN", lo, lo + 256), "B%d" % (lo // 256 % 4), V)
         else:
-            wrap("G1", 0, LR, W1, t, "B6", lst(D0))
-            wrap("G1", 0, LR, W0, 0, "B7", lst(C3))
-            gather(c("XN", *L(t - 1)), "XI", c("NXN", 32 * (t - 1), 32 * t), parts=2)
-            for lo in (0, 256):
-                gtt(c("TD", lo, lo + 256), "NFN", c("NXN", 32 * (t - 1) + lo // 16, 32 * (t - 1) + lo // 16 + 16), c("GX", lo, lo + 256), SUB)
-                tt(c("FX", *L(t - 1, lo, lo + 256)), c("SN", *L(t - 1, lo, lo + 256)), c("TD", lo, lo + 256), SUB)
+            follow("G1", "XP", lst(C2), [(W1, t, D0), (W0, 0, C3)])
+            if not OPT["xs"]:
+                gather(c("XN", *L(t - 1)), "XI", c("NXN", 32 * (t - 1), 32 * t), parts=2)
+            if YS < LR:
+                gather(c("TD", YS, LR), "NFN", c("NXN", 32 * (t - 1) + YS // 16, 32 * t), parts=2)
+                tt(c("B5", YS, LR), c("TD", YS, LR), c("B5", YS, LR), SUB, OPT["pt"])
+                tt(c("FX", *L(t - 1, YS, LR)), c("SN", *L(t - 1, YS, LR)), c("B5", YS, LR), SUB, OPT["pt"])
         pre(5, 0, lst(C2))
         pre(4, 0, lst(C3))
-        gather(c("G0"), "XN", lst(D0), parts=2)
-        wrap("G0", 0, LR, W0, 0, "B6", lst(D1))
+        follow("G0", "XN", lst(D0), [(W0, 0, D1)])
         pre(3, 1, lst(D0))
-        gather(c("G1"), "XN", lst(D1), parts=2)
-        wrap("G1", 0, LR, W0, 0, "B7", lst(D2))
+        if OPT["pend"]:
+            hint.extend(r[3] for r in recs.get("FX", []) if r[2] == "w")
+        follow("G1", "XN", lst(D1), [(W0, 0, D2)])
+        mm([(ap(c("B5")), ap(c("BS", 0, 128)), ap(c("TR", *L(t))), True, True)], LR, [c("BS"), c("TR")], [c("B5")])
+        lin(c("W0S"), c("B5"), 1.0, 0.0, "a")
+        w0 = len(ops) - 1
         pre(2, 1, lst(D1))
         if t == 0:
-            gather(c("G0"), "XN", lst(D2), parts=2)
-            wrap("G0", 0, LR, W0, 0, "B6", lst(D3))
+            follow("G0", "XN", lst(D2), [(W0, 0, D3)])
             wrap("XP", LR, V - LR, W0, 0, "B7", c("EXW", 32, 128))
             wrap("XN", 0, V, W0, 0, "B6", c("EXN"))
             for u in range(1, R):
-                sq(c("U", *L(u)), c("S", *L(u)), 1.0, -1.0)
-                lin(c("H", *L(u)), c("U", *L(u)), 0.5, 0.0)
-                dma("g", ap(c("H", *L(u))), ap(c("M", *L(u))), [c("M", *L(u)), c("H", *L(u))], [c("H", *L(u))], 3.5, after=[left], accum_op=ADD)
-        cp(c("NBU", *L(t)), c("NBI", *L(t)))
-        cp(c("NBF", *L(t)), c("NBI", *L(t)))
-        items = [(ap(c("B3")), ap(c("IDB", 0, 128)), ap(c("KC")), True, False)]
-        for k in range(K):
-            items.append((T.B3[:, k:LR:16], T.RB[:, 0:128], ap(c("NBF", t * LR + 32 * k, t * LR + 32 * k + 32)), False, False))
-        mm(items, LR + 16 * 256, [c("IDB"), c("KC"), c("RB"), c("NBF", *L(t))], [c("B3")])
+                sq(c("H", *L(u)), c("S", *L(u)), 1.0, -1.0)
+            a, a2, h = c("M", LR, V), c("U", LR, V), c("H", LR, V)
+            dma("s", ap(a2), ap(a), [a, c("EHN")], [a2], 4.5)
+            hint.extend(copies)
+            dma("g", ap(a2), ap(a), [a, a2], [a2], 5.0, accum_op=ADD)
+            dma("g", ap(h), ap(a2), [a2, h], [h], 5.0, accum_op=ADD)
+        for b in ("NBU", "NBF"):
+            hint.extend(r[3] for r in recs.get("Z", []) if r[2] == "w")
+            cp(c(b, *L(t)), c("NBI", *L(t)))
 
         early = []
         for s in range(1, 9):
@@ -463,10 +486,13 @@ def rank_program(g, core, T, topo):
                     y = c("Y", lo, hi)
                     gather(y, "FX", lst(D2, lo, hi))
                 elif s == 1:
-                    gather(c("GX", lo, hi), "NFN", lst(D3, lo, hi))
-                    gtt(c("TD", lo, hi), "NFN", lst(D2, lo, hi), c("GX", lo, hi), SUB)
-                    y = c("Y", lo, hi)
-                    gtt(y, "SN", lst(D2, lo, hi), c("TD", lo, hi), ADD)
+                    gather(part("M", 0, 3, lo, hi), "NFN", lst(D3, lo, hi), scale=-1.0)
+                    gather(part("M", 1, 3, lo, hi), "NFN", lst(D2, lo, hi))
+                    gather(part("M", 2, 3, lo, hi), "SN", lst(D2, lo, hi))
+                    y = part("O", 2, 0, lo, hi)
+                    vop(lambda lo=lo, hi=hi, k=k: vec.tensor_tensor_scan(
+                        T.O[:, 3 * lo:3 * hi], T.CQ[:, 0:3 * k], T.M[:, 9 * LR + 3 * lo:9 * LR + 3 * hi], 0.0, MUL, ADD), 3 * k,
+                        [c("CQ"), c("M", 9 * LR + 3 * lo, 9 * LR + 3 * hi)] + [part("M", j, 3, lo, hi) for j in range(3)], [y])
                 elif s < 8:
                     o = 3 * LR * (s - 2)
                     y = part("O", 2, 0, lo, hi)
@@ -479,28 +505,31 @@ def rank_program(g, core, T, topo):
                     new = c("S", *L(t, lo, hi))
                     gop(lambda new=new, y=y, k=k: g.affine_select(ap(new), ap(y), [[0, k]], GE, 0.0, 0, 0), k, [y], [new])
                     if t < R - 1:
-                        mm([(mid, T.IDB[:, 384:512], T.CP[:, 1:3 * k - 1:3], True, False), (mid, T.RB[:, 0:128], ap(y), False, True)],
-                           5 * k, [c("IDB"), c("CP"), c("RB"), y], [slot])
-                    sq(c("TB", lo, hi), y, 1.0, -1.0)
+                        mm([(T.B3[:, lo:hi], T.IDB[:, 384:512], T.CP[:, 1:3 * k - 1:3], True, False), (T.B3[:, lo:hi], T.RB[:, 0:128], ap(y), False, True)],
+                           5 * k, [c("IDB"), c("CP"), c("RB"), y], [c("B3", lo, hi)])
                     sq(c("TA", lo, hi), y)
-                    lin(b, c("TB", lo, hi), 0.5, 0.0, OPT["q2"])
-                    tt(c("H", *L(t, lo, hi)), c("TA", lo, hi), b, ADD)
-                    if t < R - 1:
-                        early.append(vop(lambda mid=mid, lo=lo, hi=hi, t=t: vec.tensor_tensor(ap(c("NF", *L(t, lo, hi))), T.TA[:, lo:hi], mid, MUL), k,
-                                         [slot, c("TA", lo, hi)], [c("NF", *L(t, lo, hi))]))
+                    sq(c("TB", lo, hi), y, 1.0, -1.0)
+                    lin(b, c("TA", lo, hi), 2.0, 0.0, OPT["q2"])
+                    tt(c("H", *L(t, lo, hi)), c("TB", lo, hi), b, ADD)
+                    if t < R - 1 and hi == LR:
+                        tt(c("NF", *L(t)), c("TA"), c("B3"), MUL)
+                        early.append(len(ops) - 1)
                     continue
+                if s == OPT["w0"] and i == 0 and t > 0:
+                    hint.append(w0)
                 if s == 3 and t > 0:
                     mm([(ap(b), T.RB[:, 16 * t:16 * t + 128], ap(y), True, True)], 4 * k, [c("RB"), y], [b])
                     y = b
                 sq(part("D1", 0, s - 1, lo, hi), y)
-                if (s, i) in OPT["peb"] and not psum(y):
+                if (s, i) in OPT["peb" if t else "peb0"] and not psum(y):
                     mm([(mid, T.IDB[:, 0:128], T.CP[:, 1:3 * k - 1:3], True, False), (mid, T.RBN[:, :], ap(y), False, True)],
                        5 * k, [c("IDB"), c("CP"), c("RBN"), y], [slot])
                 else:
-                    add([("a", ca(k), lambda mid=mid, y=y: act.activation(mid, ap(y), IDF, bias=1.5, scale=-1.0))], [y], [slot])
+                    add([("a", ca(k), lambda mid=mid, y=y: act.activation(mid, ap(y), IDF, bias=1.5, scale=-1.0))]
+                        + [("v", cv(k), lambda mid=mid, y=y: vec.tensor_scalar(mid, ap(y), -1.0, 1.5, MUL, ADD))] * (s in OPT["bv"]), [y], [slot])
         dma("s", T.ys[:, t * LR:(t + 1) * LR], ap(c("S", *L(t))), [c("S", *L(t))], [], 3.0)
         if t < R - 1:
-            cr = add([("g", 0.3, lambda t=t: g.remote_sem_update(T.sem["cr%d" % t], T.sem.lsr, spid, srid, one))], [], [c("SN"), c("NFN")],
+            cr = add([("g", 0.3, lambda t=t: g.remote_sem_update(T.sem["cr%d" % t], T.sem.lsr, spid, srid, one))], [], [c("SN"), c("NFN"), c("XN"), c("FX", *L(t))],
                      0.0, None, (), False)
             bump("lsr", 1)
             ok = event("cr%d" % t, 1, 2.0, [cr])
@@ -509,36 +538,51 @@ def rank_program(g, core, T, topo):
                                   src=ap(c(a, *L(t))), dst=ap(c(a + "N", *L(t)))) for a, m in (("S", pm_a), ("NF", pm_b))], local_sem=T.sem.lsr),
                 [c("S", *L(t)), c("NF", *L(t))], [ok])
             bump("lsr", bits(pm))
-            event("sf%d" % t, n_s, 12.0, [s_], writes=[c("SN", *L(t)), c("NFN", *L(t))])
-            dma("s", ap(c("GX")), ap(c("NFN", *L(t))), [c("NFN", *L(t))], [c("GX")])
+            event("sf%d" % t, n_s, OPT["sf"], [s_], writes=[c("SN", *L(t)), c("NFN", *L(t))])
+        if t == 0:
+            iota(c("XI"), [[16, 128], [0, 16]], 0, 0, after=[s_])
+            iota(c("CL"), [[0, 128], [1, 16]], 0, 0, after=[s_])
+            xi = [dma("s", T.XI[1:128:16, :], T.CL[0:8, :], [c("CL"), c("XI")], [("XI1", 0, 1)])]
+            xi += [dma("s", T.XI[r:128:16, :], T.XP[r:128:16, :], [c("XP"), c("XI")], [("XI%d" % r, 0, 1)]) for r in (2, 3)]
+            recs["XI"] += [(0, V, "w", i) for i in xi]
+        if t == 1:
+            iota(c("Q"), [[1, V]], 0, 0, after=[s_])
 
         def mk(k):
             return c("M", k * LR, (k + 1) * LR)
         for k in range(K + 1):
             if k < K:
                 b, u = c(WR[k % 4]), c("U", (k % URING) * LR, (k % URING + 1) * LR)
-                mm([(ap(b), ap(c("BS", 128 * k, 128 * k + 128)), ap(c("TR", *L(t))), True, True)], LR, [c("BS"), c("TR")], [b])
                 ls = c("NBU", t * LR + 32 * k, t * LR + 32 * k + 32)
-                if k < OPT["u0"]:
-                    gather((u[0], u[1], u[1] + 256), "H", (ls[0], ls[1], ls[1] + 16), "v")
-                    gather((u[0], u[1] + 256, u[2]), "H", (ls[0], ls[1] + 16, ls[2]), "a")
+                if k == 0:
+                    gtt(mk(0), "H", ls, c("W0S"), MUL)
+                    last_u = len(ops) - 1
                 else:
-                    hint.extend([last_u] if k else [])
+                    mm([(ap(b), ap(c("BS", 128 * k, 128 * k + 128)), ap(c("TR", *L(t))), True, True)], LR, [c("BS"), c("TR")], [b])
+                    hint.extend([last_u] if k > 1 else [])
                     gather(u, "H", ls, "a")
-                last_u = len(ops) - 1
-                if k == OPT["nf"]:
-                    hint.extend(early)
-                tt(mk(0) if k == 0 else b, u, b, MUL)
+                    last_u = len(ops) - 1
+                    if k == OPT["nf"]:
+                        hint.extend(early)
+                    tt(b, u, b, MUL)
+                hint.append(last_u)
+                mm([(ap(c("B3")), ap(c("IDB", 0, 128)), ap(c("KC")), True, False)] * (k == 0)
+                   + [(T.B3[:, k:LR:16], T.RB[:, 0:128], ap(c("NBF", t * LR + 32 * k, t * LR + 32 * k + 32)), False, False)],
+                   256 + LR * (k == 0), [c("IDB"), c("KC"), c("RB"), c("NBF", *L(t))], [c("B3")])
             if k >= 2:
                 b = c(WR[(k - 1) % 4])
-                tt(mk(k - 1) if k - 1 < 15 else b, mk(k - 2), b, MAX)
+                tt(mk(k - 1) if k - 1 < 15 else b, mk(k - 2), b, MAX, 2 if k >= 15 else 1)
         mf = c(WR[15 % 4])
         if t < R - 1:
-            own(t + 1, "a")
+            own(t + 1, "a", [s_])
+            if YS:
+                lin(c("B5", 0, YS), c("NF", *L(t, 0, YS)), 1.0, 0.0, "a")
+            if YS < LR:
+                lin(c("B5", YS, LR), c("NFN", *L(t, YS, LR)), 1.0, 0.0, "a")
             for u in range(R):
                 if u != t:
                     ls, fx = c("NXN" if u < t else "EXN", 32 * u, 32 * u + 32), c("FX", *L(u))
-                    add([("a", 0.065 + LR * GAT * CYC, lambda ls=ls, fx=fx: act.activation(ap(fx), ind("NFN", ls), CPY, scale=-1.0))], [c("NFN"), ls], [fx])
+                    gather(fx, "NFN", ls, "a", scale=-1.0)
                     for a in ("NFN", "SN"):
                         dma("g", ap(fx), ap(c(a, *L(u))), [c(a, *L(u)), fx], [fx], 3.5, accum_op=ADD)
                     if t == 0:
@@ -548,10 +592,10 @@ def rank_program(g, core, T, topo):
                 hint.append(last_u)
                 gather(c("XO", *L(u)), "Q", c("NXO", 32 * u, 32 * u + 32), "a")
             dma("s", T.yx[:, 0:t * LR], T.XO[0:128:16, 0:t * LR], [c("XO", 0, t * LR)], [], 2.0)
-        groups = [(k, min(k + 2, 15)) for k in range(0, 15, 2)]
+        groups = [(0, 1)] + [(k, k + 2) for k in range(1, 15, 2)]
         for j, (k0, k1) in enumerate(groups):
             for k in range(k0, k1):
-                tt(c("Z", k * LR, (k + 1) * LR), mk(k), mf, GE)
+                tt(c("Z", k * LR, (k + 1) * LR), mk(k), mf, GE, 2 if k == 0 else 1)
             cb = c(CR[j % 3], 0, 32 * (k1 - k0))
             mm([(ap(cb), T.WS[:, VB + 15 - a:VB + 143 - a], T.Z[:, k0 * LR + a:k1 * LR:16], a == 0, a == 15) for a in range(16)],
                16 * 64, [c("WS"), c("Z", k0 * LR, k1 * LR)], [cb])
@@ -562,15 +606,30 @@ def rank_program(g, core, T, topo):
                 items.append((T.B3[:, k + 1:LR:16], ap(c("IDB", 256, 384)), ap(c("CS", 32 * k, 32 * k + 32)), False, k == 14))
             mm(items, 64 * len(items), [c("IDB"), c("CS", 32 * k0, 32 * k1)], [c("B3")])
         vop(lambda: vec.tensor_tensor_scan(ap(c("BM")), ap(c("RM")), ap(c("B3")), 0.0, MUL, MAX), LR, [c("RM"), c("B3")], [c("BM")])
-        vop(lambda: vec.tensor_copy(ap(c("XA")), T.BM[:, 15:LR:16]), 32, [c("BM")], [c("XA")])
-        ts(c("XB"), c("XA"), 2047, AND)
         nx = c("NXO", 32 * t, 32 * t + 32)
+        vop(lambda: vec.tensor_scalar(ap(c("XB")), T.BM[:, 15:LR:16], 2047, None, AND), 32, [c("BM")], [c("XB")])
         cp(nx, c("XB"))
         if t < R - 1:
-            s_ = remote(lambda t=t, nx=nx: g.remote_dma(ap(c("NXN", nx[1], nx[2])), ap(nx), T.sem["nx%d" % t], T.sem.lsr, ppid, prid, pm), [nx])
-            bump("lsr", bits(pm))
-            event("nx%d" % t, n_s, OPT["nx"], [s_], writes=[c("NXN", nx[1], nx[2])])
+            def send(sem, src, dst, lat, after, local="lsr"):
+                s_ = remote(lambda: g.remote_dma(ap(dst), ap(src), T.sem[sem], T.sem[local], ppid, prid, pm), [src], after)
+                event(sem, n_s, lat, [s_], writes=[dst])
+                if local == "lsr":
+                    bump("lsr", bits(pm))
+                else:
+                    event(local, bits(pm), lat, [s_], reads=[src])
+                return [s_]
+            late = YS == LR and OPT["xs"]
+            last = [] if late else send("nx%d" % t, nx, c("NXN", nx[1], nx[2]), OPT["nx"], [])
             gather(c("XP", *L(t)), "XI", nx, parts=2)
+            if OPT["xs"]:
+                last = send("xp%d" % t, c("XP", *L(t)), c("XN", *L(t)), OPT["nx"] + 0.2, last)
+            if YS:
+                gather(c("TD", 0, YS), "NF", (nx[0], nx[1], nx[1] + YS // 16), parts=2)
+                tt(c("B5", 0, YS), c("TD", 0, YS), c("B5", 0, YS), SUB, OPT["pt"])
+                tt(c("TB", 0, YS), c("S", *L(t, 0, YS)), c("B5", 0, YS), SUB, OPT["pt"])
+                last = send("yp%d" % t, c("TB", 0, YS), c("FX", *L(t, 0, YS)), OPT["nx"] + OPT["yl"], last, "yl%d" % t)
+                if late and t < R - 2:
+                    send("nx%d" % t, nx, c("NXN", nx[1], nx[2]), OPT["nx"] + 1, last)
         else:
             gather(c("XO", *L(t)), "Q", nx, parts=2)
             dma("s", T.yx[:, t * LR:V], T.XO[0:128:16, t * LR:V], [c("XO", *L(t))], [], 2.0)

from concourse.bass import DstId, RemoteDMATransfer
from concourse.mybir import AluOpType, ActivationFunctionType

V, K, R, LR = 2048, 16, 4, 512
NEAR, FAR, DIRECT = 0, 1, 2
SENDS = [[(0, 256, FAR, 11.0)], [(256, 768, FAR, 11.0)], [], [(768, 1024, FAR, 11.0), (1024, 1280, DIRECT, 7.0)],
         [(1280, 1792, DIRECT, 8.0)], [(1792, 2048, DIRECT, 8.5)]]
LOADS = [(0, 256), (256, 256), (256, 768), (768, 1280), (1280, 1792), (1792, 2048)]
URING = 6
CH = [(0, 128), (128, 256), (256, 384), (384, 512)]
F32, BF, I32, U16 = "float32", "bfloat16", "int32", "uint16"

SCRATCH = {}
for _n in ("S", "NF", "H", "SN", "NFN", "FX", "Q", "XO", "NBF"):
    SCRATCH[_n] = ("sbuf", [128, V], F32)
for _n in ("XI", "XP", "XN", "CL", "TR", "BS"):
    SCRATCH[_n] = ("sbuf", [128, V], BF)
for _n in ("Y", "TA", "TB", "TD"):
    SCRATCH[_n] = ("sbuf", [128, LR], F32)
SCRATCH["BM"] = ("sbuf", [128, LR], I32)
for _n in ("G0", "G1", "EH", "EHN", "SP", "KC", "RM", "CS", "IDB", "W0S"):
    SCRATCH[_n] = ("sbuf", [128, LR], BF)
for _n in ("EXW", "EXN", "NXO", "NXN"):
    SCRATCH[_n] = ("sbuf", [128, 128], U16)
SCRATCH.update({
    "NBI": ("sbuf", [128, V], I32), "NBU": ("sbuf", [128, V], U16),
    "U": ("sbuf", [128, URING * LR], F32), "M": ("sbuf", [128, 15 * LR], F32), "Z": ("sbuf", [128, 15 * LR], BF),
    "D1": ("sbuf", [128, 6 * 3 * LR], F32), "O": ("sbuf", [128, 3 * LR], F32),
    "LS": ("sbuf", [128, 6 * 32], U16), "EC": ("sbuf", [128, LR], I32), "WS": ("sbuf", [128, 768], BF),
    "I0": ("sbuf", [128, 176], I32), "I1": ("sbuf", [128, 80], I32), "RB": ("sbuf", [128, 176], F32),
    "RBN": ("sbuf", [128, 128], F32), "CP": ("sbuf", [128, 384], BF), "C15": ("sbuf", [128, 256], BF), "CQ": ("sbuf", [128, 384], BF),
    "XB": ("sbuf", [128, 32], I32),
})
for _b in range(8):
    SCRATCH["B%d" % _b] = ("psum", [128, 512], F32)

NDMA = 48
SEMAPHORES = (["cv", "ca", "cp", "cg", "lsi", "lsr", "aeh"] + ["d%d" % j for j in range(NDMA)]
              + [s + str(j) for s in ("ad", "hh") for j in range(8)]
              + [s + str(t) for s in ("sf", "nx", "cr", "xp", "yp", "yl") for t in range(R - 1)])

ADD, SUB, MUL, MAX = AluOpType.add, AluOpType.subtract, AluOpType.mult, AluOpType.max
AND, SHR, EQ, GE = AluOpType.bitwise_and, AluOpType.arith_shift_right, AluOpType.is_equal, AluOpType.is_ge
SQ, IDF, CPY = ActivationFunctionType.Square, ActivationFunctionType.Identity, ActivationFunctionType.Copy

CYC, PEC, GAT, HOP = 0.83e-3, 0.6e-3, 1.65, 0.19
OPT = dict(hl=[(0, 512)], first=-1.0, step=1.5, pp=2, fb=40, q2="av", on={}, nx=2.6, peb=[(s, i) for s in range(1, 7) for i in range(4) if (s + i) % 2 == 0], peb0=[(s, i) for s in range(1, 7) for i in range(4) if (s + i) % 2 == 0], xnd=1, bv=(), cv=1, pt=1, sf=9.5, xs=1, ys=320, yl=0.8, eh=4.5, pend=0, w0=6, u0=0, nf=2, seed=1, amp=0.6, win=3.0, fpe=0, npe=0)
PLAN = []


def bits(m):
    return bin(m).count("1")


def helpers_of(c, dst, T, topo):
    free = [h for h in topo.cores_of(c) if T.rank_of(h) is None and topo.may_write(h, dst) and topo.addr(h)[2] != topo.addr(c)[2]]
    hs = [[h for h in free if topo.die(h) == topo.die(c)][0], [h for h in free if topo.die(h) != topo.die(c)][0]]
    ways = {p[2] for call in SENDS for p in call}
    es = [e for e in topo.engines(c, hs[0]) if DIRECT not in ways or e not in topo.engines(c, dst)]
    a, b = (es[0::2], es[1::2]) if {NEAR, FAR} <= ways else (es, es)
    return hs, [sum(1 << e for e in a), sum(1 << e for e in b), topo.mask(c, dst)]


def helper_program(g, core, way, n_in, dst, T, topo):
    rid, pid, _ = topo.addr(dst)
    m = topo.mask(core, dst)
    mine = [(j, p) for j, p in enumerate(p for call in SENDS for p in call) if p[2] == way]
    for j, (lo, hi, _, _) in mine:
        g.wait_ge(T.sem["hh%d" % j], n_in)
        g.remote_dma(T.SN[:, lo:hi], T.S[:, lo:hi], T.sem["ad%d" % j], T.sem.lsi, pid, rid, m)
    if mine:
        g.wait_ge(T.sem.lsi, len(mine) * bits(m))


def lay_out(ops):
    for o in ops:
        o["rest"] = o["lat"]
    for o in reversed(ops):
        o["rank"] = min(c for _, c, _ in o["opts"]) + o["rest"]
        for d in o["deps"]:
            ops[d]["rest"] = max(ops[d]["rest"], ops[d]["lat"] + HOP + o["rank"])
        for d in o["behind"]:
            ops[d]["rest"] = max(ops[d]["rest"], o["rank"])

    def place(busy, e, t, c):
        for s, f in busy.setdefault(e, []) if e != "x" else []:
            if s >= t + c - 1e-9:
                break
            t = max(t, f)
        return t

    def take(busy, e, t, c):
        if e != "x":
            busy[e].append((t, t + c))
            busy[e].sort()

    def hop(a, b):
        return 0 if a == b == "p" else HOP

    def forward():
        busy = {}
        for o in sorted(ops, key=lambda o: (-round(o["rank"], 6), o["id"])):
            best = None
            for e, c, fn in o["opts"]:
                t = place(busy, e, max([ops[d]["end"] + hop(e, ops[d]["eng"]) for d in o["deps"]]
                                       + [ops[d]["end"] - ops[d]["lat"] for d in o["behind"]] + [0]), c)
                if best is None or t + c < best[0] - 1e-9:
                    best = (t + c, t, e, fn, c)
            o["start"], o["eng"], o["fn"], o["cost"], o["end"] = best[1], best[2], best[3], best[4], best[0] + o["lat"]
            take(busy, o["eng"], o["start"], o["cost"])
        return max(o["end"] for o in ops)

    def backward():
        busy = {}
        for o in ops:
            o["rest"] = o["lat"]
        for o in sorted(ops, key=lambda o: (-round(o["start"] + o["cost"], 6), -o["id"])):
            t = place(busy, o["eng"], o["rest"], o["cost"])
            take(busy, o["eng"], t, o["cost"])
            o["rank"] = t + o["cost"]
            for d in o["deps"]:
                ops[d]["rest"] = max(ops[d]["rest"], ops[d]["lat"] + hop(o["eng"], ops[d]["eng"]) + o["rank"])
            for d in o["behind"]:
                ops[d]["rest"] = max(ops[d]["rest"], o["rank"])

    if not PLAN:
        best, seed = None, OPT["seed"]
        for n in range(OPT["fb"] + 1):
            span = forward()
            if best is None or span < best[0]:
                best = (span, [(o["start"], o["eng"]) for o in ops], [(o["cost"], o["end"]) for o in ops])
            if n % 2:
                for o, (s, e), (c, f) in zip(ops, best[1], best[2]):
                    o["start"], o["eng"], o["cost"], o["end"] = s, e, c, f
            backward()
            if n % 2:
                seed = (seed * 1103515245 + 12345) % 2147483648
                t0 = best[0] * seed / 2147483648
                for o in reversed(ops):
                    seed = (seed * 1103515245 + 12345) % 2147483648
                    o["rank"] = max(o["rank"] + (OPT["amp"] * (seed / 2147483648 - 0.5) if t0 < o["start"] < t0 + OPT["win"] else 0), o.get("floor", 0))
                    for d in o["deps"] + o["behind"]:
                        ops[d]["floor"] = max(ops[d].get("floor", 0), o["rank"] + 1e-3)
                for o in ops:
                    o["floor"] = 0
        PLAN.extend(best[1])
        OPT["span"] = best[0]
    for o, (s, e) in zip(ops, PLAN):
        o["start"], o["eng"], o["fn"] = s, e, [fn for q, _, fn in o["opts"] if q == e][0]
    return sorted(ops, key=lambda o: (o["start"], o["id"]))


def rank_program(g, core, T, topo):
    rank = T.rank_of(core)
    n = len(T.cores)
    if rank is None:
        for r in range(n):
            hs, ms = helpers_of(T.cores[r], T.cores[(r - 1) % n], T, topo)
            if core in hs:
                h = hs.index(core)
                helper_program(g, core, h, bits(ms[h]), T.cores[(r - 1) % n], T, topo)
        return
    pred, succ = T.cores[(rank - 1) % n], T.cores[(rank + 1) % n]
    hs, hm = helpers_of(core, pred, T, topo)
    hid = [DstId(rid=topo.addr(h)[0], pnc=topo.addr(h)[1]) for h in hs + [pred]]
    prid, ppid, _ = topo.addr(pred)
    srid, spid, _ = topo.addr(succ)
    pm = topo.mask(core, pred)
    pe = topo.engines(core, pred)
    pm_a = sum(1 << e for e in pe[:len(pe) // 2])
    pm_b = pm & ~pm_a
    n_s = bits(topo.mask(succ, core))
    n_h = [bits(topo.mask(h, core)) for h in helpers_of(succ, core, T, topo)[0] + [succ]]
    one = 1 << topo.engines(core, succ)[0]
    vec, act, pe_ = g.vector, g.scalar, g.tensor
    Qs = {"v": vec, "a": act, "p": pe_, "g": g, "s": g.sync}

    ops, recs, bank, total, ndma = [], {}, {}, {}, [0]
    hint = []

    def psum(r):
        return r[0][0] == "B" and r[0][1:].isdigit()

    def add(opts, reads, writes, lat=0.0, tok="own", after=(), record=True):
        i = len(ops)
        behind = list(hint)
        del hint[:]
        deps = set(after)
        for (b, lo, hi) in reads:
            deps |= {r[3] for r in recs.get(b, []) if r[2] == "w" and r[0] < hi and lo < r[1]}
        for (b, lo, hi) in writes:
            deps |= {r[3] for r in recs.get(b, []) if r[0] < hi and lo < r[1]}
        who = opts[0][0] if len(opts) == 1 else i
        for b in {r[0] for r in reads + writes if psum(r)}:
            w, cur, old = bank.get(b, (None, [], []))
            if w == who:
                deps |= set(old)
                cur.append(i)
            else:
                deps |= set(cur)
                bank[b] = (who, [i], cur)
        if record:
            for (b, lo, hi) in writes:
                recs[b] = [r for r in recs.get(b, []) if not (lo <= r[0] and r[1] <= hi)] + [(lo, hi, "w", i)]
            for (b, lo, hi) in reads:
                recs.setdefault(b, []).append((lo, hi, "r", i))
        ops.append({"id": i, "opts": opts, "deps": sorted(deps), "behind": behind, "lat": lat, "tok": tok})
        return i

    def bump(s, k):
        total[s] = total.get(s, 0) + k
        return (s, total[s])

    def dma(e, o, i, reads, writes, lat=2.5, after=(), **kw):
        s = "d%d" % ndma[0]
        ndma[0] += 1
        return add([(e, 0.6 if e == "g" else 0.05, lambda: Qs[e].dma_start(o, i, **kw).then_inc(T.sem[s], 16))], reads, writes, lat, bump(s, 16), after)

    def remote(fn, reads, after=(), cost=0.3):
        return add([("g", cost, fn)], reads, [], 0.0, None, after, False)

    def event(sem, k, lat, after, reads=(), writes=()):
        return add([("x", lat, None)], list(reads), list(writes), 0.0, bump(sem, k), after)

    def c(b, lo=0, hi=None):
        return (b, lo, SCRATCH[b][1][1] if hi is None else hi)

    def part(nm, j, s, lo=0, hi=LR):
        return ("@%s.%d.%d" % (nm, j, s), lo, hi)

    def ap(r):
        b, lo, hi = r
        if b[0] == "@":
            nm, j, s = b[1:].split(".")
            o = 3 * LR * int(s) + int(j)
            return T[nm][:, o + 3 * lo:o + 3 * hi - 2:3]
        return T[b][:, lo:hi]

    def w(r):
        return r[2] - r[1]

    def cv(k):
        return 0.01 + max(64, k) * CYC

    def ca(k):
        return 0.015 + max(64, k) * CYC

    def vop(fn, k, reads, writes, **kw):
        return add([("v", cv(k), fn)], reads, writes, **kw)

    def gop(fn, k, reads, writes, **kw):
        return add([("g", 0.14 + 2 * k * CYC, fn)], reads, writes, **kw)

    def tt(o, a, b, f, parts=1):
        for p in range(parts):
            h = w(o) // parts
            oo, aa, bb = [(r[0], r[1] + p * h, r[1] + (p + 1) * h) for r in (o, a, b)]
            vop(lambda oo=oo, aa=aa, bb=bb: vec.tensor_tensor(ap(oo), ap(aa), ap(bb), f), h * (1 if psum(a) or psum(b) else 2), [aa, bb], [oo])

    def ts(o, a, s1, f0, oap=None):
        vop(lambda: vec.tensor_scalar(oap if oap is not None else ap(o), ap(a), s1, None, f0), w(a), [a], [o])

    def cp(o, a):
        vop(lambda: vec.tensor_copy(ap(o), ap(a)), w(o), [a], [o])

    def sq(o, a, bias=0.0, scale=1.0):
        add([("a", ca(w(o)), lambda: act.activation(ap(o), ap(a), SQ, bias=bias, scale=scale))], [a], [o])

    def lin(o, a, scale, bias, on="av"):
        opts = {"a": ("a", ca(w(o)), lambda: act.activation(ap(o), ap(a), IDF, bias=bias, scale=scale)),
                "v": ("v", cv(w(o)), lambda: vec.tensor_scalar(ap(o), ap(a), scale, bias, MUL, ADD))}
        add([opts[e] for e in on], [a], [o])

    def ind(tab, ls):
        return T[tab][:, 0:V].indirect(ap(ls))

    def gather(o, tab, ls, on="av", parts=1, scale=1.0):
        for p in range(parts):
            h, k = w(o) // parts, w(ls) // parts
            oo, ll = (o[0], o[1] + p * h, o[1] + (p + 1) * h), (ls[0], ls[1] + p * k, ls[1] + (p + 1) * k)
            opts = {"a": ("a", 0.065 + h * GAT * CYC, lambda oo=oo, ll=ll: act.activation(ap(oo), ind(tab, ll), CPY, scale=scale)),
                    "v": ("v", 0.05 + h * GAT * CYC, lambda oo=oo, ll=ll: vec.tensor_copy(ap(oo), ind(tab, ll)) if scale == 1.0 else
                          vec.tensor_scalar(ap(oo), ind(tab, ll), scale, None, MUL))}
            add([opts[e] for e in on], [c(tab), ll], [oo])

    def gtt(o, tab, ls, b, f):
        add([("v", 0.05 + w(o) * 2 * CYC, lambda: vec.tensor_tensor(ap(o), ind(tab, ls), ap(b), f))], [c(tab), ls, b], [o])

    def mm(items, cyc, reads, writes):
        def fn():
            last = None
            for o, l, r, st, sp in items:
                last = pe_.matmul(o, l, r, st, sp)
            return last
        add([("p", cyc * PEC, fn)], reads, writes)

    W0, W1, VB = 0, 256, 512

    def wrap(src, lo, width, sel, rot, b, dst):
        k = width // 16
        items = []
        for a in range(16):
            s = sel + (15 - a - 16 * rot) % 128
            items.append((T[b][:, 0:k], T.WS[:, s:s + 128], T[src][:, lo + a:lo + width:16], a == 0, a == 15))
        mm(items, 16 * max(64, k), [c(src, lo, lo + width), c("WS", sel, sel + 256)], [c(b, 0, k)])
        cp(dst, c(b, 0, k))

    def L(t, lo=0, hi=LR):
        return (t * LR + lo, t * LR + hi)

    def lst(i, lo=0, hi=LR):
        return c("LS", 32 * i + lo // 16, 32 * i + hi // 16)
    C2, C3, D0, D1, D2, D3 = range(6)

    def c1(t):
        return c("EXW", 32 * t, 32 * t + 32)

    def iota(o, pattern, base, cm, after=()):
        kw = {} if o[0] in ("I0", "I1") else {"allow_small_or_imprecise_dtypes": True}
        return gop(lambda: g.iota(ap(o), pattern, base, cm, **kw), w(o), [], [o], after=after)

    for x, (lo, hi) in enumerate(LOADS):
        hint.extend(range(len(ops)))
        if lo == hi:
            for q in range(4):
                dma("sa"[q % 2], T.EC[32 * q:32 * q + 32, :], (T.ex, T.pt)[q % 2][:], [], [("EC%d" % q, 0, 1)], 2.0 + lo / 800)
        else:
            dma("s", T.S[:, lo:hi], T.sat[:, lo:hi], [], [c("S", lo, hi)], 1.9 + hi / 800)
    iota(c("I1", 0, 32), [[-1, 4], [-4, 8]], 0, 1)
    iota(c("I1", 32, 48), [[0, 2], [-16, 8]], 0, 1)
    iota(c("I0"), [[1, 176]], 0, -1)
    vop(lambda: vec.memset(ap(c("SP")), 0.0), 256, [], [c("SP")])
    vop(lambda: vec.memset(ap(c("WS")), 0.0), 384, [], [c("WS")])
    for q in range(4):
        ts(c("SP"), c("I1", 0, 32), float(32 * q), EQ, T.SP[:, (0, 2, 1, 3)[q]:LR:16])
    ts(c("I1", 48, 64), c("I1", 32, 48), 1, SHR)
    ts(c("I1", 64, 80), c("I1", 32, 48), 4, SHR)
    ts(c("WS", W0, W0 + 256), c("I1", 48, 64), 0.0, EQ, T.WS[:, W0 + 15:W0 + 256:16])
    ts(c("WS", W1, W1 + 256), c("I1", 48, 64), 1.0, EQ, T.WS[:, W1 + 15:W1 + 256:16])
    ts(c("WS", VB, VB + 256), c("I1", 64, 80), 0.0, EQ, T.WS[:, VB + 15:VB + 256:16])
    ecs = [("EC%d" % q, 0, 1) for q in range(4)]
    vop(lambda: vec.tensor_scalar(T.EH[:, :], T.EC[:, :], 1.0, None, MUL), LR, ecs, [c("EH")])
    vop(lambda: vec.tensor_tensor(T.EH[64:128, :], T.EC[64:128, :], T.EH[64:128, :], SUB), 2 * LR, ecs + [c("EH")], [c("EH")])

    def spread(dst, src):
        for a in range(4):
            b = c("B%d" % a)
            mm([(ap(b), T.SP[:, 128 * a:128 * a + 128], ap(c(src)), True, True)], LR, [c("SP"), c(src)], [b])
            lin(c(dst, *L(a)), b, 1.0, 0.0)
    spread("XP", "EH")
    sends, pieces = [], []
    for call in SENDS:
        if not call:
            sends.append(remote(lambda: g.remote_dma(ap(c("EHN")), ap(c("EH")), T.sem.aeh, T.sem.lsr, ppid, prid, pm), [c("EH")], sends[-1:], 0.3 if sends else 1.5))
            bump("lsr", bits(pm))
            event("aeh", n_s, OPT["eh"], sends[-1:], writes=[c("EHN")])
            continue
        mine = list(enumerate(call, len(pieces)))
        pieces += call
        s_ = remote(lambda mine=mine: g.remote_dma_fused(
            [RemoteDMATransfer(dst_ids=[hid[h]], dma_engine_mask=hm[h], remote_sem=T.sem[("ad%d" if h == DIRECT else "hh%d") % j],
                               src=T.S[:, lo:hi], dst=T["SN" if h == DIRECT else "S"][:, lo:hi]) for j, (lo, hi, h, _) in mine],
            local_sem=T.sem.lsi), [c("S", p[0], p[1]) for p in call], sends[-1:], 0.5 if sends else 1.5)
        sends.append(s_)
        for j, (lo, hi, h, lat) in mine:
            event("ad%d" % j, n_h[h], lat + OPT["first"], [s_], writes=[c("SN", lo, hi)])
    left = event("lsi", sum(bits(hm[p[2]]) for p in pieces), 5.0, sends, reads=[c("S")])
    wrap("XP", 0, LR, W0, 0, "B6", c1(0))

    ts(c("RB", 0, 128), c("I0", 0, 128), 0.0, EQ)
    ts(c("RB", 128, 176), c("I0", 128, 176), 128.0, EQ)
    for i, s in enumerate((1.0, 32768.0, -32768.0, -1.0)):
        lin(c("IDB", 128 * i, 128 * i + 128), c("RB", 0, 128), s, 0.0)
    vop(lambda: vec.memset(ap(c("C15")), 1.5), 128, [], [c("C15")])

    def ftab(src, dst, r, b, keep, pe=False):
        lo, hi = r[1], r[2]
        sq(c("M", keep + lo, keep + hi), c(src, lo, hi))
        if pe:
            for x in range(0, hi - lo, 256):
                mm([(T[b][:, x:x + 256], T.IDB[:, 384:512], T.C15[:, :], True, False), (T[b][:, x:x + 256], T.RB[:, 0:128], T[src][:, lo + x:lo + x + 256], False, True)],
                   5 * 256, [c("IDB"), c("C15"), c("RB"), c(src, lo, hi)], [c(b, x, x + 256)])
        else:
            lin(c(b, 0, hi - lo), c(src, lo, hi), 1.0, -1.5)
        tt(c(dst, lo, hi), c("M", keep + lo, keep + hi), c(b, 0, hi - lo), MUL)

    for i, u in enumerate((0, 1, 2, 3)):
        ftab("S", "NF", c("S", *L(u)), "B%d" % (4 + i % 2), 0, i < OPT["fpe"])
    lin(c("RBN"), c("RB", 0, 128), -1.0, 0.0)
    for j, s in enumerate((0.0, 1.5, 1.0)):
        vop(lambda j=j, s=s: vec.memset(T.CP[:, j:384:3], s), 64, [], [c("CP")])
    vop(lambda: vec.memset(ap(c("CQ")), 1.0), 192, [], [c("CQ")])
    vop(lambda: vec.memset(T.CQ[:, 0:384:3], 0.0), 64, [], [c("CQ")])
    hint.append(iota(c("XN"), [[0, V]], 0, 0, after=sends))
    iota(c("BS"), [[0, V]], 1, 0, after=sends)
    bs = gop(lambda: g.affine_select(ap(c("BS")), ap(c("BS")), [[-1, 16], [-16, 8], [0, 16]], EQ, 0.0, 0, 1), V, [c("BS")], [c("BS")])
    iota(c("KC"), [[0, 32], [-2048, 16]], 30720, 0, after=[bs])
    vop(lambda: vec.memset(T.KC[:, 15:LR:16], 524288.0), 32, [], [c("KC")])
    vop(lambda: vec.memset(ap(c("RM")), 1.0), 256, [], [c("RM")])
    vop(lambda: vec.memset(T.RM[:, 0:LR:16], 0.0), 32, [], [c("RM")])

    YS = OPT["ys"]
    WR = ["B5", "B6", "B7", "B4"]
    SB = ["B0", "B1", "B2", "B4"]
    CR = ["B0", "B1", "B2"]

    def pre(s, far, ls, on="av"):
        a, b = OPT["on"].get(s, (on, on))
        gather(part("D1", 1, s - 2), ("NF", "NFN")[far], ls, a, OPT["pp"])
        gather(part("D1", 2, s - 2), ("S", "SN")[far], ls, b, OPT["pp"])

    def own(t, on, behind=()):
        pre(6, 0, c1(t), on)
        for j, a in ((1, c("NF", *L(t))), (2, c("S", *L(t)))):
            hint.extend(behind)
            gop(lambda j=j, a=a: g.affine_select(ap(part("D1", j, 5)), ap(a), [[0, LR]], GE, 0.0, 0, 0), LR, [a], [part("D1", j, 5)])

    for t in range(R):
        HL = OPT["hl"] if t else [(0, LR)]
        begun = [r[3] for r in recs.get("NXO", []) if r[2] == "w"] if OPT["cv"] else []

        def follow(buf, tab, src, outs):
            for h, (lo, hi) in enumerate(HL):
                gather(c(buf, lo, hi), tab, (src[0], src[1] + lo // 16, src[1] + hi // 16), parts=2)
                for x, (sel, rot, dst) in enumerate(outs):
                    wrap(buf, lo, hi - lo, sel, rot, (("B6", "B7") if x == 0 or t == 0 else ("B0", "B1"))[h], lst(dst, lo, hi))
        follow("G0", "XP", c1(t), [(W0, 0, C2)])
        if t == 0:
            follow("G1", "XP", lst(C2), [(W0, 0, C3)])
            follow("G0", "XP", lst(C3), [(W1, 0, D0)])
            if OPT["xnd"]:
                xs = [dma("s", T.XN[r:128:16, :], T.EHN[64 * r:64 * r + 32, :], [c("EHN"), c("XN")], [("XN%d" % r, 0, 1)], 1.8) for r in range(2)]
                recs["XN"] += [(0, V, "w", i) for i in xs]
            else:
                spread("XN", "EHN")
            own(0, "av")
            copies = [len(ops) - 2, len(ops) - 1]
            for b, lo, hi, lat in (("TR", 0, V, 4.0), ("NBI", 0, LR, 2.5), ("NBI", LR, V, 6.0)):
                hint.extend(xs)
                dma("s", ap(c(b, lo, hi)), (T.tr if b == "TR" else T.nb)[:, lo:hi], [], [c(b, lo, hi)], lat, after=[left])
            for j, p in enumerate(sorted(pieces, key=lambda p: p[3] + 0.3 * pieces.index(p))):
                for lo in range(p[0], p[1], 256):
                    ftab("SN", "NFN", c("SN", lo, lo + 256), "B%d" % (lo // 256 % 4), V)
        else:
            follow("G1", "XP", lst(C2), [(W1, t, D0), (W0, 0, C3)])
            if not OPT["xs"]:
                gather(c("XN", *L(t - 1)), "XI", c("NXN", 32 * (t - 1), 32 * t), parts=2)
            if YS < LR:
                gather(c("TD", YS, LR), "NFN", c("NXN", 32 * (t - 1) + YS // 16, 32 * t), parts=2)
                tt(c("B5", YS, LR), c("TD", YS, LR), c("B5", YS, LR), SUB, OPT["pt"])
                tt(c("FX", *L(t - 1, YS, LR)), c("SN", *L(t - 1, YS, LR)), c("B5", YS, LR), SUB, OPT["pt"])
        pre(5, 0, lst(C2))
        pre(4, 0, lst(C3))
        follow("G0", "XN", lst(D0), [(W0, 0, D1)])
        pre(3, 1, lst(D0))
        if OPT["pend"]:
            hint.extend(r[3] for r in recs.get("FX", []) if r[2] == "w")
        follow("G1", "XN", lst(D1), [(W0, 0, D2)])
        mm([(ap(c("B5")), ap(c("BS", 0, 128)), ap(c("TR", *L(t))), True, True)], LR, [c("BS"), c("TR")], [c("B5")])
        lin(c("W0S"), c("B5"), 1.0, 0.0, "a")
        w0 = len(ops) - 1
        pre(2, 1, lst(D1))
        if t == 0:
            follow("G0", "XN", lst(D2), [(W0, 0, D3)])
            wrap("XP", LR, V - LR, W0, 0, "B7", c("EXW", 32, 128))
            wrap("XN", 0, V, W0, 0, "B6", c("EXN"))
            for u in range(1, R):
                sq(c("H", *L(u)), c("S", *L(u)), 1.0, -1.0)
            a, a2, h = c("M", LR, V), c("U", LR, V), c("H", LR, V)
            dma("s", ap(a2), ap(a), [a, c("EHN")], [a2], 4.5)
            hint.extend(copies)
            dma("g", ap(a2), ap(a), [a, a2], [a2], 5.0, accum_op=ADD)
            dma("g", ap(h), ap(a2), [a2, h], [h], 5.0, accum_op=ADD)
        for b in ("NBU", "NBF"):
            hint.extend(r[3] for r in recs.get("Z", []) if r[2] == "w")
            cp(c(b, *L(t)), c("NBI", *L(t)))

        early = []
        for s in range(1, 9):
            for i, (lo, hi) in enumerate(CH):
                k = hi - lo
                b, slot, mid = c(SB[i], LR - k, LR), c(SB[i], 0, 3 * k), T[SB[i]][:, 1:3 * k - 1:3]
                if s == 1:
                    mm([(ap(slot), T.IDB[:, 0:128], T.CP[:, 0:3 * k], True, True)], 3 * k, [c("IDB"), c("CP")], [slot])
                if s == 1 and t > 0:
                    y = c("Y", lo, hi)
                    gather(y, "FX", lst(D2, lo, hi))
                elif s == 1:
                    gather(part("M", 0, 3, lo, hi), "NFN", lst(D3, lo, hi), scale=-1.0)
                    gather(part("M", 1, 3, lo, hi), "NFN", lst(D2, lo, hi))
                    gather(part("M", 2, 3, lo, hi), "SN", lst(D2, lo, hi))
                    y = part("O", 2, 0, lo, hi)
                    vop(lambda lo=lo, hi=hi, k=k: vec.tensor_tensor_scan(
                        T.O[:, 3 * lo:3 * hi], T.CQ[:, 0:3 * k], T.M[:, 9 * LR + 3 * lo:9 * LR + 3 * hi], 0.0, MUL, ADD), 3 * k,
                        [c("CQ"), c("M", 9 * LR + 3 * lo, 9 * LR + 3 * hi)] + [part("M", j, 3, lo, hi) for j in range(3)], [y])
                elif s < 8:
                    o = 3 * LR * (s - 2)
                    y = part("O", 2, 0, lo, hi)
                    vop(lambda o=o, lo=lo, hi=hi, slot=slot: vec.tensor_tensor_scan(
                        T.O[:, 3 * lo:3 * hi], ap(slot), T.D1[:, o + 3 * lo:o + 3 * hi], 0.0, MUL, ADD), 3 * k,
                        [slot] + [part("D1", j, s - 2, lo, hi) for j in range(3)], [y])
                else:
                    continue
                if s == 7:
                    new = c("S", *L(t, lo, hi))
                    gop(lambda new=new, y=y, k=k: g.affine_select(ap(new), ap(y), [[0, k]], GE, 0.0, 0, 0), k, [y], [new])
                    if t < R - 1:
                        mm([(T.B3[:, lo:hi], T.IDB[:, 384:512], T.CP[:, 1:3 * k - 1:3], True, False), (T.B3[:, lo:hi], T.RB[:, 0:128], ap(y), False, True)],
                           5 * k, [c("IDB"), c("CP"), c("RB"), y], [c("B3", lo, hi)])
                    sq(c("TA", lo, hi), y)
                    sq(c("TB", lo, hi), y, 1.0, -1.0)
                    lin(b, c("TA", lo, hi), 2.0, 0.0, OPT["q2"])
                    tt(c("H", *L(t, lo, hi)), c("TB", lo, hi), b, ADD)
                    if t < R - 1 and hi == LR:
                        tt(c("NF", *L(t)), c("TA"), c("B3"), MUL)
                        early.append(len(ops) - 1)
                    continue
                if s == OPT["w0"] and i == 0 and t > 0:
                    hint.append(w0)
                if s == 3 and t > 0:
                    mm([(ap(b), T.RB[:, 16 * t:16 * t + 128], ap(y), True, True)], 4 * k, [c("RB"), y], [b])
                    y = b
                sq(part("D1", 0, s - 1, lo, hi), y)
                if (s, i) in OPT["peb" if t else "peb0"] and not psum(y):
                    mm([(mid, T.IDB[:, 0:128], T.CP[:, 1:3 * k - 1:3], True, False), (mid, T.RBN[:, :], ap(y), False, True)],
                       5 * k, [c("IDB"), c("CP"), c("RBN"), y], [slot])
                else:
                    add([("a", ca(k), lambda mid=mid, y=y: act.activation(mid, ap(y), IDF, bias=1.5, scale=-1.0))]
                        + [("v", cv(k), lambda mid=mid, y=y: vec.tensor_scalar(mid, ap(y), -1.0, 1.5, MUL, ADD))] * (s in OPT["bv"]), [y], [slot])
        dma("s", T.ys[:, t * LR:(t + 1) * LR], ap(c("S", *L(t))), [c("S", *L(t))], [], 3.0)
        if t < R - 1:
            cr = add([("g", 0.3, lambda t=t: g.remote_sem_update(T.sem["cr%d" % t], T.sem.lsr, spid, srid, one))], [], [c("SN"), c("NFN"), c("XN"), c("FX", *L(t))],
                     0.0, None, (), False)
            bump("lsr", 1)
            ok = event("cr%d" % t, 1, 2.0, [cr])
            s_ = remote(lambda t=t: g.remote_dma_fused([
                RemoteDMATransfer(dst_ids=[DstId(rid=prid, pnc=ppid)], dma_engine_mask=m, remote_sem=T.sem["sf%d" % t],
                                  src=ap(c(a, *L(t))), dst=ap(c(a + "N", *L(t)))) for a, m in (("S", pm_a), ("NF", pm_b))], local_sem=T.sem.lsr),
                [c("S", *L(t)), c("NF", *L(t))], [ok])
            bump("lsr", bits(pm))
            event("sf%d" % t, n_s, OPT["sf"], [s_], writes=[c("SN", *L(t)), c("NFN", *L(t))])
        if t == 0:
            iota(c("XI"), [[16, 128], [0, 16]], 0, 0, after=[s_])
            iota(c("CL"), [[0, 128], [1, 16]], 0, 0, after=[s_])
            xi = [dma("s", T.XI[1:128:16, :], T.CL[0:8, :], [c("CL"), c("XI")], [("XI1", 0, 1)])]
            xi += [dma("s", T.XI[r:128:16, :], T.XP[r:128:16, :], [c("XP"), c("XI")], [("XI%d" % r, 0, 1)]) for r in (2, 3)]
            recs["XI"] += [(0, V, "w", i) for i in xi]
        if t == 1:
            iota(c("Q"), [[1, V]], 0, 0, after=[s_])

        def mk(k):
            return c("M", k * LR, (k + 1) * LR)
        for k in range(K + 1):
            if k < K:
                b, u = c(WR[k % 4]), c("U", (k % URING) * LR, (k % URING + 1) * LR)
                ls = c("NBU", t * LR + 32 * k, t * LR + 32 * k + 32)
                if k == 0:
                    gtt(mk(0), "H", ls, c("W0S"), MUL)
                    last_u = len(ops) - 1
                else:
                    mm([(ap(b), ap(c("BS", 128 * k, 128 * k + 128)), ap(c("TR", *L(t))), True, True)], LR, [c("BS"), c("TR")], [b])
                    hint.extend([last_u] if k > 1 else [])
                    gather(u, "H", ls, "a")
                    last_u = len(ops) - 1
                    if k == OPT["nf"]:
                        hint.extend(early)
                    tt(b, u, b, MUL)
                hint.append(last_u)
                mm([(ap(c("B3")), ap(c("IDB", 0, 128)), ap(c("KC")), True, False)] * (k == 0)
                   + [(T.B3[:, k:LR:16], T.RB[:, 0:128], ap(c("NBF", t * LR + 32 * k, t * LR + 32 * k + 32)), False, False)],
                   256 + LR * (k == 0), [c("IDB"), c("KC"), c("RB"), c("NBF", *L(t))], [c("B3")])
            if k >= 2:
                b = c(WR[(k - 1) % 4])
                tt(mk(k - 1) if k - 1 < 15 else b, mk(k - 2), b, MAX, 2 if k >= 15 else 1)
        mf = c(WR[15 % 4])
        if t < R - 1:
            own(t + 1, "a", [s_])
            if YS:
                lin(c("B5", 0, YS), c("NF", *L(t, 0, YS)), 1.0, 0.0, "a")
            if YS < LR:
                lin(c("B5", YS, LR), c("NFN", *L(t, YS, LR)), 1.0, 0.0, "a")
            for u in range(R):
                if u != t:
                    ls, fx = c("NXN" if u < t else "EXN", 32 * u, 32 * u + 32), c("FX", *L(u))
                    gather(fx, "NFN", ls, "a", scale=-1.0)
                    for a in ("NFN", "SN"):
                        dma("g", ap(fx), ap(c(a, *L(u))), [c(a, *L(u)), fx], [fx], 3.5, accum_op=ADD)
                    if t == 0:
                        gather(c("XP", *L(u)), "XI", c1(u), "a")
        else:
            for u in range(t):
                hint.append(last_u)
                gather(c("XO", *L(u)), "Q", c("NXO", 32 * u, 32 * u + 32), "a")
            dma("s", T.yx[:, 0:t * LR], T.XO[0:128:16, 0:t * LR], [c("XO", 0, t * LR)], [], 2.0)
        groups = [(0, 1)] + [(k, k + 2) for k in range(1, 15, 2)]
        for j, (k0, k1) in enumerate(groups):
            for k in range(k0, k1):
                tt(c("Z", k * LR, (k + 1) * LR), mk(k), mf, GE, 2 if k == 0 else 1)
            cb = c(CR[j % 3], 0, 32 * (k1 - k0))
            mm([(ap(cb), T.WS[:, VB + 15 - a:VB + 143 - a], T.Z[:, k0 * LR + a:k1 * LR:16], a == 0, a == 15) for a in range(16)],
               16 * 64, [c("WS"), c("Z", k0 * LR, k1 * LR)], [cb])
            lin(c("CS", 32 * k0, 32 * k1), cb, 1.0, 0.0, "a")
            items = []
            for k in range(k0, k1):
                items.append((T.B3[:, k:LR:16], ap(c("IDB", 128, 256)), ap(c("CS", 32 * k, 32 * k + 32)), False, False))
                items.append((T.B3[:, k + 1:LR:16], ap(c("IDB", 256, 384)), ap(c("CS", 32 * k, 32 * k + 32)), False, k == 14))
            mm(items, 64 * len(items), [c("IDB"), c("CS", 32 * k0, 32 * k1)], [c("B3")])
        vop(lambda: vec.tensor_tensor_scan(ap(c("BM")), ap(c("RM")), ap(c("B3")), 0.0, MUL, MAX), LR, [c("RM"), c("B3")], [c("BM")])
        nx = c("NXO", 32 * t, 32 * t + 32)
        vop(lambda: vec.tensor_scalar(ap(c("XB")), T.BM[:, 15:LR:16], 2047, None, AND), 32, [c("BM")], [c("XB")])
        cp(nx, c("XB"))
        if t < R - 1:
            def send(sem, src, dst, lat, after, local="lsr"):
                s_ = remote(lambda: g.remote_dma(ap(dst), ap(src), T.sem[sem], T.sem[local], ppid, prid, pm), [src], after)
                event(sem, n_s, lat, [s_], writes=[dst])
                if local == "lsr":
                    bump("lsr", bits(pm))
                else:
                    event(local, bits(pm), lat, [s_], reads=[src])
                return [s_]
            late = YS == LR and OPT["xs"]
            last = [] if late else send("nx%d" % t, nx, c("NXN", nx[1], nx[2]), OPT["nx"], [])
            gather(c("XP", *L(t)), "XI", nx, parts=2)
            if OPT["xs"]:
                last = send("xp%d" % t, c("XP", *L(t)), c("XN", *L(t)), OPT["nx"] + 0.2, last)
            if YS:
                gather(c("TD", 0, YS), "NF", (nx[0], nx[1], nx[1] + YS // 16), parts=2)
                tt(c("B5", 0, YS), c("TD", 0, YS), c("B5", 0, YS), SUB, OPT["pt"])
                tt(c("TB", 0, YS), c("S", *L(t, 0, YS)), c("B5", 0, YS), SUB, OPT["pt"])
                last = send("yp%d" % t, c("TB", 0, YS), c("FX", *L(t, 0, YS)), OPT["nx"] + OPT["yl"], last, "yl%d" % t)
                if late and t < R - 2:
                    send("nx%d" % t, nx, c("NXN", nx[1], nx[2]), OPT["nx"] + 1, last)
        else:
            gather(c("XO", *L(t)), "Q", nx, parts=2)
            dma("s", T.yx[:, t * LR:V], T.XO[0:128:16, t * LR:V], [c("XO", *L(t))], [], 2.0)

    known = {e: {} for e in Qs}
    for o in lay_out(ops):
        e = o["eng"]
        if e == "x":
            o["clock"] = dict([o["tok"]])
            continue
        for d in sorted(o["deps"], key=lambda d: -ops[d]["start"]):
            p = ops[d]
            if p["tok"] is None or e == p["eng"] == "p" or known[e].get(p["tok"][0], 0) >= p["tok"][1]:
                continue
            Qs[e].wait_ge(T.sem[p["tok"][0]], p["tok"][1])
            for s, v in p["clock"].items():
                known[e][s] = max(known[e].get(s, 0), v)
        ins = o["fn"]()
        if o["tok"] == "own":
            o["tok"] = bump("c" + e, 1)
            ins.then_inc(T.sem["c" + e], 1)
        if o["tok"] is not None:
            o["clock"] = dict(known[e], **dict([o["tok"]]))
    for s in sorted(total):
        g.wait_ge(T.sem[s], total[s])
